import numpy as np, ml_dtypes
CORES = [40,41,42,43,44,45,46,47]
N = 8
BF = ml_dtypes.bfloat16
def gentries(a):
    return np.ascontiguousarray(a.reshape(8, 16, -1).transpose(0, 2, 1)).reshape(8, -1)
def gtable(e):
    e = np.asarray(e); return np.ascontiguousarray(e.reshape(8, -1, 16).transpose(0, 2, 1)).reshape(128, -1).astype(np.int32)
PN, NT, ND, L, V, ST, H = 4096, 1024, 512, 256, 3, 3, 3
def parts(rng):
    prog = rng.integers(0, 16, (N, 8, 16, PN)); eff = rng.integers(0, 16, (N, 8, 16, ND)); x = rng.integers(0, 16, (N, 8, 16, L)); goal = rng.integers(0, 16, (N, 8, 16, L))
    wt = rng.integers(0, 256, (N, 8, 16)); team = rng.integers(0, PN, (N, 8, 16, NT)); start = rng.integers(0, NT, (N, 8, L))
    hub = rng.integers(0, NT, (8, 12)); gi = np.arange(8)[None, :, None]; u = rng.random((N, 8, PN))
    act = np.where(u < 0.4, rng.integers(0, NT, u.shape), np.where(u < 0.65, hub[gi, rng.integers(0, 12, u.shape)], NT + rng.integers(0, ND, u.shape)))
    start = np.where(rng.random(start.shape) < 0.3, hub[gi, rng.integers(0, 12, start.shape)], start)
    return [prog, act, team, eff, x, goal, wt, start]
def pack(p):
    prog, act, team, eff, x, goal, wt, start = p
    def b(a): return np.ascontiguousarray(a.reshape(N, 128, -1)).astype(np.float32).astype(BF)
    def i(a): return np.ascontiguousarray(a.reshape(N, 128, -1)).astype(np.int32)
    return {"prog": b(prog), "act": np.ascontiguousarray(act).astype(np.int32), "team": i(team), "eff": b(eff), "x0": b(x), "goal": b(goal), "wt": i(wt), "start": np.stack([gtable(a) for a in start])}
def setup_inputs(rng):
    p = parts(rng); prog, act, team, eff, x, goal, wt, start = p
    for q in range(N):
        for g in range(8):
            t = rng.permutation(NT)[:2]; j = rng.permutation(L)[:6]
            team[q, g][:, t] = 0; act[q, g, 0] = t[0]; start[q, g, j[:3]] = t[0]; start[q, g, j[3:]] = t[1]
    return pack(p)
def setup_inputs_corners(rng):
    p = parts(rng); prog, act, team, eff, x, goal, wt, start = p
    for q in range(N):
        for g in range(8):
            m = (g + q) % 8
            if m == 0: act[q, g] = rng.integers(0, NT, PN)
            elif m == 1: act[q, g] = NT + rng.integers(0, ND, PN); goal[q, g] = x[q, g]
            elif m == 2: act[q, g] = rng.choice(np.array([0, NT - 1]), PN); start[q, g] = rng.choice(np.array([0, NT - 1, 1, NT - 2]), L)
            elif m == 3:
                t = int(rng.choice(np.array([0, NT - 1, NT // 2]))); act[q, g] = t; start[q, g, ::2] = t
            elif m == 4:
                start[q, g] = NT - 1; team[q, g, :, NT - 1] = 0
                act[q, g] = np.where(rng.random(PN) < 0.5, rng.integers(1, 9, PN), NT + rng.integers(0, ND, PN)); act[q, g, 0] = 0
            elif m == 5:
                act[q, g] = NT + rng.integers(0, ND, PN); eff[q, g] = 7; goal[q, g] = np.abs(x[q, g] - 7); team[q, g] = rng.choice(np.array([0, 1, PN - 2, PN - 1]), (16, NT))
            elif m == 6: prog[q, g] = prog[q, g, :, :1].copy(); wt[q, g] = 255 * rng.integers(0, 2, 16)
            else: eff[q, g, :, ::2] = 0; wt[q, g] = 0; x[q, g, :, ::4] = 0; x[q, g, :, 1::4] = 15
    return pack(p)
def two(rng, hi, n):
    return hi * np.where(rng.random((N, 8, 1, n)) < 0.5, rng.integers(0, 2, (N, 8, 1, n)), rng.integers(0, 2, (N, 8, 16, n)))
def setup_inputs_ends(rng):
    prog = two(rng, 15, PN); eff = two(rng, 15, ND); x = two(rng, 15, L); goal = two(rng, 15, L); wt = 255 * rng.integers(0, 2, (N, 8, 16))
    team = np.where(rng.random((N, 8, 16, NT)) < 0.8, two(rng, PN - 1, NT), rng.integers(0, PN, (N, 8, 16, NT)))
    s = (N, 8, PN); far = np.where(rng.random(s) < 0.5, rng.choice(np.array([1, NT - 1, NT, NT + ND - 2]), s), rng.integers(0, NT + ND, s))
    act = np.where(rng.random(s) < 0.75, (NT + ND - 1) * rng.integers(0, 2, s), far)
    s = (N, 8, L); start = np.where(rng.random(s) < 0.8, (NT - 1) * rng.integers(0, 2, s), rng.integers(0, NT, s))
    a6 = act[:, 6]; a6[a6 == NT - 1] = NT
    start[:, 6] = np.where(rng.random((N, L)) < 0.75, 0, rng.integers(1, NT - 1, (N, L))); start[:, 6, L - 1] = NT - 1
    wt[:, 6] = 0; wt[:, 6, 1::2] = 255; wt[:, 6, 0] = 17; x[:, 6, ::2, L - 1] = 15; x[:, 6, 1::2, L - 1] = 0; goal[:, 6, :, L - 1] = x[:, 6, :, L - 1]
    team[:, 6, :, NT - 1] = PN - 1; act[:, 6, ((((PN - 1) * 511) >> 5) + PN - 1) & (PN - 1)] = NT + ND - 1; eff[:, 6, :, ND - 1] = 15
    c = np.arange(PN); c = int(np.flatnonzero((((c >> 5) + c) & (PN - 1)) == PN - 1)[0])
    wt[:, 7] = 255; prog[:, 7, :, 0] = 15; prog[:, 7, :, PN - 1] = 15; team[:, 7, :, NT - 1] = 0; team[:, 7, 0, NT - 1] = c
    act[:, 7, PN - 1] = NT + ND - 1; act[:, 7, 0] = NT; eff[:, 7, :, ND - 1] = 15; eff[:, 7, :, 0] = 0
    x[:, 7, :, L - 1] = 0; goal[:, 7, :, L - 1] = 15; x[:, 7, :, L - 2] = 0; goal[:, 7, :, L - 2] = 0; x[:, 7, :, 0] = 15; goal[:, 7, :, 0] = 0
    start[:, 7, L - 2:] = NT - 1; start[:, 7, 0] = NT - 1
    x[:, 5, :, L - 1] = 0; goal[:, 5] = x[:, 5]; goal[:, 5, :, L - 1] = 15; start[:, 5, L - 1] = NT // 2
    team[:, 5, :, NT // 2] = c; team[:, 5, :, 0] = 0; team[:, 5, :, NT - 1] = PN - 1
    act[:, 5, PN - 1] = 0; act[:, 5, 0] = NT - 1; act[:, 5, (((PN - 1) >> 5) + PN - 1) & (PN - 1)] = NT + ND - 1; eff[:, 5, :, ND - 1] = 15
    return pack([prog, act, team, eff, x, goal, wt, start])
def setup_inputs_full(rng):
    p = parts(rng); prog, act, team, eff, x, goal, wt, start = p
    keys = np.array([3, 7, 11, 15]); c = np.arange(PN)
    same = np.stack([np.flatnonzero(((13 * c + 97 * int(e) + 1) & (PN - 1)) == c)[:4] for e in keys])
    for q in range(N):
        for g in range(8):
            m = (0, 1, 2, 3, 4, 1, 3, 0)[g]; S = rng.permutation(NT); o = rng.permutation(PN - PN // 16); n = o + (o >> 5)
            if m == 0:
                act[q, g] = NT + rng.integers(0, ND, PN); start[q, g] = S[:L]; eff[q, g] = 0; eff[q, g, :8] = 2
                x[q, g, :8] = rng.integers(2 * V, 16, (8, L)); near = np.argsort(rng.random((8, L)), axis=0) < rng.permutation(np.arange(L) % 5)[None, :]
                goal[q, g, :8] = x[q, g, :8] - 2 * V + 2 * near; goal[q, g, :8, int(rng.integers(0, L))] = 15
            elif m == 1:
                wt[q, g] = 0; start[q, g] = S[:L]; x[q, g] = rng.integers(8, 16, (16, L)); goal[q, g] = 0; eff[q, g] = rng.integers(0, 8, (16, ND)); eff[q, g, 0] = np.maximum(eff[q, g, 0], 1)
                act[q, g, n[:4 * L]] = S[L + rng.integers(0, L, 4 * L)]; act[q, g, n[4 * L:8 * L]] = S[2 * L + rng.integers(0, L, 4 * L)]; act[q, g, n[8 * L:12 * L]] = NT + rng.integers(0, ND, 4 * L)
                team[q, g][:, S[:L]] = o[:4 * L].reshape(4, L)[rng.integers(0, 4, (16, L)), np.arange(L)[None, :]]
                team[q, g][:, S[L:2 * L]] = o[4 * L + rng.integers(0, 4 * L, (16, L))]; team[q, g][:, S[2 * L:3 * L]] = o[8 * L + rng.integers(0, 4 * L, (16, L))]
            elif m == 2:
                act[q, g] = NT + rng.integers(0, ND, PN); start[q, g] = S[:L]; goal[q, g] = x[q, g]; eff[q, g] = np.maximum(eff[q, g], 1)
            elif m == 3:
                h = L // 4; j = rng.permutation(L); a, b = j[:h], j[h:2 * h]; ab = j[:2 * h]
                start[q, g] = S[rng.integers(2 * h, NT, L)]; start[q, g, ab] = S[:2 * h]; x[q, g][:, ab] = 0; goal[q, g][:, ab] = 15
                d = rng.permutation(ND)[:2]; eff[q, g, :, d[0]] = 15; eff[q, g, :, d[1]] = 0; eff[q, g, int(rng.integers(0, 16)), d[1]] = 1
                prog[q, g, :, n[0]] = 15; prog[q, g, :, n[1]] = 15; prog[q, g, int(rng.integers(0, 16)), n[1]] = 14; prog[q, g][:, n[2:2 + h]] = 0
                act[q, g, n[0]] = NT + d[0]; act[q, g, n[1]] = NT + d[1]; act[q, g, n[2:2 + h]] = S[h:2 * h]
                team[q, g][:, S[:2 * h]] = o[0]; team[q, g][rng.integers(1, 16, h), S[:h]] = o[1]
                team[q, g][rng.integers(0, 16, h) * rng.permutation(np.arange(h) % 2), S[h:2 * h]] = o[2:2 + h]
            else:
                h = L // 2; j = np.sort(rng.permutation(L).reshape(h, 2), axis=1); w = rng.integers(0, 4, h)
                wt[q, g] = 0; wt[q, g, 0] = 1; act[q, g] = NT + rng.integers(0, ND, PN); eff[q, g] = np.maximum(eff[q, g], 1); eff[q, g, 0] = 0
                x[q, g, 0, j[:, 0]] = keys[w]; x[q, g, 0, j[:, 1]] = 2 * rng.integers(0, 8, h); goal[q, g] = x[q, g]
                start[q, g, j[:, 0]] = S[:h]; start[q, g, j[:, 1]] = S[:h]; team[q, g][:, S[:h]] = same[w[None, :], rng.integers(0, same.shape[1], (16, h))]
    return pack(p)
def setup_inputs_spread(rng):
    def v(n): return rng.integers(0, 16, (N, 8, 16, n)) >> rng.integers(0, 4, (N, 8, 1, n))
    def w(n, shape):
        k = rng.choice(np.array([0.5, 1.0, 2.0, 3.0]), (N, 8) + (1,) * (len(shape) - 2)); return np.minimum((n * rng.random(shape) ** k).astype(np.int64), n - 1)
    return pack([v(PN), w(NT + ND, (N, 8, PN)), w(PN, (N, 8, 16, NT)), v(ND), v(L), v(L), w(256, (N, 8, 16)), w(NT, (N, 8, L))])
def setup_inputs_ties(rng):
    p = parts(rng); prog, act, team, eff, x, goal, wt, start = p
    pat = rng.integers(0, 3, (N, 8, 16, 32)); prog = np.take_along_axis(pat, rng.integers(0, 32, (N, 8, 1, PN)), 3)
    eff = rng.integers(0, 3, eff.shape); x = rng.integers(0, 3, x.shape); goal = rng.integers(0, 3, goal.shape)
    team[:, :, 8:, ::2] = team[:, :, :8, ::2]
    return pack([prog, act, team, eff, x, goal, wt, start])
def check_inputs(d):
    bad = []
    for k, lo, hi in (("prog", 0, 15), ("act", 0, NT + ND - 1), ("team", 0, PN - 1), ("eff", 0, 15), ("x0", 0, 15), ("goal", 0, 15), ("wt", 0, 255), ("start", 0, NT - 1)):
        a = np.asarray(d[k]).astype(np.float64)
        if not (np.min(a) >= lo and np.max(a) <= hi): bad.append("range of " + k)
        elif np.any(a != np.floor(a)): bad.append("whole numbers in " + k)
    return bad
def nums(a, n):
    return a.astype(np.float32).astype(np.int32).reshape(N, 8, 16, n)
def reference(prog, act, team, eff, x0, goal, wt, start):
    P = nums(prog, PN); D = nums(eff, ND); x = nums(x0, L); z = nums(goal, L); w = nums(wt, 1)
    T = team.astype(np.int64).reshape(N, 8, 16, NT); a = act.astype(np.int64)
    s = np.stack([gentries(t) for t in start]).astype(np.int64); A = np.zeros((N, 8), np.int64)
    for v in range(V):
        nx = np.zeros_like(x); ns = np.zeros_like(s)
        for r in range(N):
            q = (r + H * v) % N; X = x[r]; Y = X; cur = s[r]; trail = [cur]
            e = np.add.reduce(w[q] * X, axis=1).astype(np.int64) & 255
            go = np.ones((8, L), bool); won = np.zeros((8, L), bool); lastk = np.zeros((8, L), np.int64); lastt = np.zeros((8, L), np.int64); first = lastk
            for i in range(ST):
                c = np.take_along_axis(T[q], cur[:, None, :], 2)
                n = (((c * (2 * e[:, None, :] + 1)) >> 5) + c) & (PN - 1)
                d = np.take_along_axis(P[q], n.reshape(8, 1, 16 * L), 2).reshape(8, 16, 16, L) - X[:, :, None, :]
                score = np.add.reduce(d * d, axis=1)
                ak = np.take_along_axis(a[q], n.reshape(8, 16 * L), 1).reshape(8, 16, L)
                bar = np.zeros((8, 16, L), bool)
                for t in trail: bar = bar | (ak == t[:, None, :])
                k = np.argmin(np.where(bar, 1000000, score), axis=1)
                ok = go & ~np.all(bar, axis=1)
                an = np.take_along_axis(ak, k[:, None, :], 1)[:, 0]
                if i == 0: first = np.take_along_axis(n, k[:, None, :], 1)[:, 0]
                lastk = np.where(ok, k, lastk); lastt = np.where(ok, cur, lastt); won = won | ok
                fin = ok & (an >= NT); j = np.where(fin, an - NT, 0)
                Y = np.where(fin[:, None, :], np.abs(X - np.take_along_axis(D[q], j[:, None, :], 2)), Y)
                go = ok & ~fin; cur = np.where(go, an, cur); trail.append(cur)
            old = np.add.reduce(np.abs(X - z[r]), axis=1); new = np.add.reduce(np.abs(Y - z[r]), axis=1)
            good = new < old - (A[q] & 7)[:, None]
            up = good & (cur != s[r]); fail = won & ~good
            for g in range(8):
                j = np.flatnonzero(up[g]); u, ix = np.unique(first[g, j], return_index=True); a[q, g, u] = cur[g, j[ix]]
                j = np.flatnonzero(fail[g]); u, ix = np.unique(lastt[g, j], return_index=True); j = j[ix]; k = lastk[g, j]
                T[q, g, k, u] = (13 * T[q, g, k, u] + 97 * e[g, j] + 1) & (PN - 1)
            A[q] = A[q] + np.add.reduce(good.astype(np.int64), axis=1)
            nx[r] = Y; ns[r] = cur
        x, s = nx, ns
    return {"yteam": T.reshape(N, 128, NT).astype(np.float32), "yact": a.astype(np.float32), "yx": x.reshape(N, 128, L).astype(np.float32).astype(BF)}

@@ -1,0 +1,746 @@
+from concourse.bass import DstId, RemoteDMATransfer
+from concourse.mybir import AluOpType as A, AxisListType, ActivationFunctionType as F
+
+NV, HOP = 3, 3
+CFG = {"GA": 1.56, "SCA": 3.8, "PEC": 0.45, "WAKE": 130.0, "FIX": 0.0, "DM": 1.0,
+       "CV": (512, 256, 256, 256, 256, 256), "CS": (1536, 512), "XG": 10, "PEN": 2000.0, "PENS": 1000.0,
+       "SLACK": {"v": 0.0, "s": 300.0, "t": 0.0}, "SEED": 6, "NOISE": 300.0,
+       "SPD": 0, "SPA": 1, "FBI": 6, "ORD": 1, "PF": 256, "PENP": 3000.0, "MXS": 0, "TTS": 0, "DLS": 1, "XR0": 0, "MM": 4, "VAR": (1,), "BARFIRST": 0,
+       "TOV": ("Wb", "col", "cm", "Wd", "t8", "Wt", "Wl", "In", "IB", "I32", "mk64", "Y1", "Wa", "xr")}
+CY = 0.83
+MAGIC = 6442450944.0
+
+
+def _scratch():
+    s = {}
+
+    def sb(n, c, d):
+        s[n] = ("sbuf", [128, c], d)
+    for n, c in (("pg", 4096), ("meta", 4224), ("D", 4096), ("M", 4096), ("xr", 4096), ("ef", 544), ("cm", 1024), ("qc", 512),
+                 ("Wd", 32), ("Wm", 32), ("Wa", 24), ("Wt", 128), ("Wl", 8), ("kc", 768), ("ones", 128), ("IB", 128),
+                 ("I32", 128), ("Ip", 128), ("In", 128), ("Wb", 128), ("Q", 144), ("Ya", 144), ("Wdd", 1024),
+                 ("S1m", 128), ("S2m", 128), ("rmin", 512), ("rsum", 80), ("rs16", 128), ("e0", 40), ("b8", 8), ("b8m", 8),
+                 ("x0s", 256), ("x1s", 256), ("x2s", 256), ("x3s", 256), ("z0", 256), ("z1", 256), ("z2", 256),
+                 ("xo0", 256), ("xo1", 256), ("xo2", 256), ("tc", 768), ("ab", 768), ("bar", 768), ("Pr", 1024), ("oz", 256),
+                 ("tt", 256), ("mx", 256), ("good", 48), ("eq", 2048), ("sp", 256), ("G1", 256), ("G2", 256), ("av", 256)):
+        sb(n, c, "bfloat16")
+    for n, c in (("Lb", 256), ("ex", 384)):
+        sb(n, c, "float16")
+    for n, c in (("tm", 1160), ("idt", 5256), ("actf", 4224), ("ic", 256), ("R128", 128), ("B128", 128), ("t128", 256),
+                 ("D128", 128), ("mk1", 192), ("mk64", 128), ("col", 24), ("pw", 128), ("thr", 128), ("E", 256), ("Er", 512),
+                 ("sc", 1024), ("T", 96), ("x1", 80), ("g1", 80), ("go", 96), ("w", 80), ("p12", 160), ("S1", 160),
+                 ("ok", 80), ("okk", 96), ("v", 80), ("p34", 160), ("Fb", 320), ("pre", 160), ("kl", 16), ("Y0", 32),
+                 ("Y1", 32), ("Zc", 16), ("kcol", 256), ("us", 256), ("cold", 256), ("c13", 256), ("df", 256), ("dl", 256),
+                 ("t8", 64)):
+        sb(n, c, "float32")
+    for n, c in (("ti", 1024), ("ai", 256), ("pi", 512), ("wi", 1), ("si", 16), ("ci", 8), ("vi", 256), ("ni", 256),
+                 ("mi", 320), ("pay", 320), ("kk", 80), ("A7", 8), ("ui", 256), ("u2", 256)):
+        sb(n, c, "int32")
+    for n, c in (("nu", 256), ("cl0", 256), ("cl1", 256), ("cl2", 256), ("co0", 256), ("co1", 256), ("co2", 256),
+                 ("cs", 32), ("O", 72), ("lst", 128)):
+        sb(n, c, "uint16")
+    for n in ("K0", "K1", "A0", "A1", "C0", "C1", "B0", "B1"):
+        s[n] = ("psum", [128, 512], "float32")
+    return s
+
+
+SCRATCH = _scratch()
+NDMA = 30
+SEMAPHORES = ["sv", "ss", "st", "sg", "ls", "rz"] + ["r%d%d" % (v, h) for v in range(NV) for h in range(2)] + \
+    ["d%d" % i for i in range(NDMA)]
+PSUM = ("K0", "K1", "A0", "A1", "C0", "C1", "B0", "B1")
+_ORDER = {}
+
+
+def build(core, T, topo):
+    rank = T.rank_of(core)
+    n = len(T.cores)
+    ops = []
+    nd = [0]
+    last = {}
+    GA, SCA, PEC, FIX, DM = CFG["GA"], CFG["SCA"], CFG["PEC"], CFG["FIX"], CFG["DM"]
+
+    def S(name, lo=None, hi=None, step=None, p=None):
+        t = T[name]
+        if lo is None:
+            lo, hi = 0, t.shape[1]
+        ps = slice(None) if p is None else p
+        ap = t[ps, lo:hi] if step is None else t[ps, lo:hi:step]
+        cnt = (hi - lo + (step or 1) - 1) // (step or 1)
+        return (ap, ((name, lo, hi),), cnt, t.dtype)
+
+    def IND(win, off):
+        return (win[0].indirect(off[0]), win[1] + off[1], off[2] * 16, "ind")
+
+    def add(eng, fn, rd, wr, cost, key=None, kind="c", sem=None, lat=0.0, after=None, pen=0.0):
+        r, w = [], []
+        for x in rd:
+            r += list(x[1])
+        for x in wr:
+            w += list(x[1])
+        ops.append({"e": eng, "fn": fn, "r": r, "w": w, "c": cost + (FIX if eng in "vs" else 0.0), "key": key, "k": kind,
+                    "sem": sem, "lat": lat, "after": after, "pen": pen, "ord": last.get(eng) if pen else None})
+        if pen:
+            last[eng] = len(ops) - 1
+        return len(ops) - 1
+
+    def two(x):
+        return "16" in str(x[3])
+
+    def aps(xs):
+        return [x for x in xs if isinstance(x, tuple)]
+
+    def a0(x):
+        return x[0] if isinstance(x, tuple) else x
+
+    def vcost(out, in0, base):
+        if in0[3] == "ind":
+            return 50 + in0[2] * GA * CY
+        if out[3] == "ind":
+            return 50 + out[2] * SCA * CY
+        return max(64, base) * CY
+
+    def tt(out, a, b, op, pen=0.0):
+        ps = a[1][0][0] in PSUM or b[1][0][0] in PSUM
+        add("v", lambda e: e.tensor_tensor(out[0], a[0], b[0], op), [a, b] + ([out] if out[3] == "ind" else []), [out],
+            vcost(out, a, a[2] * (1 if ps else 2)), pen=pen)
+
+    early = [True]
+
+    def ts(out, a, s1, op0, s2=None, op1=None, key=None):
+        c = vcost(out, a, a[2] * (0.5 if two(a) and two(out) else 1))
+        if op1 is None:
+            add("v", lambda e: e.tensor_scalar(out[0], a[0], a0(s1), None, op0), aps([a, s1]), [out], c, key=key)
+        else:
+            add("v", lambda e: e.tensor_scalar(out[0], a[0], a0(s1), a0(s2), op0, op1), aps([a, s1, s2]), [out], c, key=key)
+
+    def cp(out, a):
+        add("v", lambda e: e.tensor_copy(out[0], a[0]), [a] + ([out] if out[3] == "ind" else []), [out],
+            vcost(out, a, a[2] * (0.5 if two(a) and two(out) else 1)))
+
+    def ms(out, c):
+        add("v", lambda e: e.memset(out[0], c), [], [out], max(64, out[2] * (0.5 if two(out) else 1)) * CY)
+
+    def scan(out, d0, d1, init, op0, op1):
+        add("v", lambda e: e.tensor_tensor_scan(out[0], d0[0], d1[0], init, op0, op1), [d0, d1], [out], max(64, out[2]) * CY)
+
+    def act(out, a, f=F.Identity, bias=0.0, scale=1.0, key=None, pen=0.0):
+        if early[0] and f == F.Identity and out[1][0][0] in CFG["TOV"]:
+            return ts(out, a, scale, A.mult, bias, A.add, key=key)
+        c = 65 + a[2] * GA * CY if a[3] == "ind" else max(64, a[2]) * CY + 20
+        add("s", lambda e: e.activation(out[0], a[0], f, bias=a0(bias), scale=a0(scale)), aps([a, bias, scale]), [out], c, key=key, pen=pen)
+
+    def iota(out, pat, base, cm):
+        if "int" in str(out[3]):
+            add("g", lambda e: e.iota(out[0], pat, base, cm), [], [out], 130 + 2 * CY * out[2])
+        else:
+            add("g", lambda e: e.iota(out[0], pat, base, cm, allow_small_or_imprecise_dtypes=True), [], [out], 130 + 2 * CY * out[2])
+
+    def sel(out, a, pat, op, fill, base, cm, key=None):
+        add("g", lambda e: e.affine_select(out[0], a[0], pat, op, fill, base, cm), [a], [out], 170 + 2 * CY * out[2], key=key)
+
+    def mm(lst, start=True, stop=True):
+        m = CFG["MM"]
+        if len(lst) > m:
+            for q in range(0, len(lst), m):
+                mm(lst[q:q + m], start and q == 0, stop and q + m >= len(lst))
+            return
+
+        def fn(e):
+            for i, (o, l, r) in enumerate(lst):
+                ins = e.matmul(o[0], l[0], r[0], start and i == 0, stop and i == len(lst) - 1)
+            return ins
+        add("t", fn, [x[1] for x in lst] + [x[2] for x in lst], [x[0] for x in lst],
+            sum(max(min(64, x[1][2]), x[2][2]) for x in lst) * PEC, lat=60.0)
+
+    def dma(out, in_, q="y", key=None, lat=2000.0):
+        sem = "d%d" % nd[0]
+        nd[0] += 1
+        o = out if isinstance(out, tuple) else (out, (), 0, 0)
+        i = in_ if isinstance(in_, tuple) else (in_, (), 0, 0)
+        add(q, lambda e: e.dma_start(o[0], i[0]), [i], [o], 60.0, key=key, kind="d", sem=(sem, 16), lat=lat * DM)
+
+    def send(pairs, sem, cnt):
+        def fn(e):
+            trs = []
+            for j, (src, dst, r) in enumerate(pairs):
+                c = T.cores[r % n]
+                en = topo.engines(core, c)
+                per = len(en) // len(pairs)
+                m = 0
+                for x in en[j * per:(j + 1) * per]:
+                    m |= 1 << x
+                rid, pid, _ = topo.addr(c)
+                trs.append(RemoteDMATransfer(dst_ids=[DstId(rid=rid, pnc=pid)], dma_engine_mask=m, remote_sem=T.sem[sem], src=src[0], dst=dst[0]))
+            return e.remote_dma_fused(trs, local_sem=T.sem.ls)
+        i = add("g", fn, [x[0] for x in pairs], [], 600.0, kind="s")
+        add("r", None, [], [x[1] for x in pairs], 0.0, kind="r", sem=(sem, cnt), lat=1500.0 * DM, after=i)
+
+    NE = len(topo.engines(core, T.cores[(rank + HOP) % n]))
+    p1 = slice(0, 1)
+
+    dma(S("x0s"), T.x0[:])
+    dma(S("wi"), T.wt[:], q="s")
+    dma(S("ai"), T.act[:], q="s")
+    dma(S("si"), T.start[:], q="s")
+    for c in range(4):
+        dma(S("pg", 1024 * c, 1024 * c + 1024), T.prog[:, 1024 * c:1024 * c + 1024], lat=2600.0 + 800 * c)
+    dma(S("ti"), T.team[:], lat=5800.0)
+    dma(S("z0"), T.goal[:], lat=5800.0)
+    ms(S("ef"), 0.0)
+    dma(S("ef", 16, 528), T.eff[:], lat=5800.0)
+
+    iota(S("ci", 0, 1), [[0, 1]], 0, 1)
+    iota(S("R128"), [[-16, 8], [0, 16]], 0, 1)
+    iota(S("ic"), [[1, 256]], 0, 0)
+    R8 = S("R128", 0, 128, 16)
+    ms(S("meta", 0, 4096), 0.0)
+    ts(S("ci", 1, 2), S("ci", 0, 1), 15, A.bitwise_and)
+    ts(S("ci", 2, 3), S("ci", 0, 1), 4, A.arith_shift_right)
+    ts(S("ci", 3, 4), S("ci", 0, 1), 3, A.arith_shift_right, 1, A.bitwise_and)
+    cp(S("col", 0, 4), S("ci", 0, 4))
+    col = lambda i: S("col", i, i + 1)
+    pc, lc, bc, hc = col(0), col(1), col(2), col(3)
+    ts(col(4), S("wi"), 2.0, A.mult)
+    ts(S("t128", 0, 128), S("R128"), -0.5, A.is_gt)
+    ts(S("t128", 128, 256), S("R128"), 15.5, A.is_lt)
+    tt(S("B128"), S("t128", 0, 128), S("t128", 128, 256), A.mult)
+    B8 = S("B128", 0, 128, 16)
+    act(S("Wb"), S("B128"), scale=col(4))
+    cp(S("cl0", 0, 8), S("si", 0, 8))
+    cp(S("cl0", 128, 136), S("si", 8, 16))
+    cp(S("tm", 128, 1152), S("ti"))
+    act(col(5), hc, bias=8.0, scale=64.0)
+    act(col(6), bc, bias=col(5), scale=8.0)
+    ts(S("Q"), S("ic", 0, 144), col(6), A.is_equal)
+    ts(S("pi", 0, 256), S("ai"), 63, A.bitwise_and)
+    ts(S("pi", 256, 512), S("ai"), 6, A.arith_shift_right)
+    cp(S("cm", 0, 512), S("pi"))
+    iota(S("cm", 512, 768), [[0, 4], [1, 64]], 0, 0)
+    iota(S("df"), [[1, 4], [0, 64]], 0, 0)
+    act(col(7), lc, scale=4.0)
+    act(S("cm", 768, 1024), S("df"), bias=col(7))
+    for r in (2, 3, 0, 1):
+        dma(S("meta", 0, 4096, p=slice(2 + r, 128, 16)), S("cm", 256 * r, 256 * r + 256), key="meta")
+    for c in range(8):
+        act(S("M", 512 * c, 512 * c + 512), S("pg", 512 * c, 512 * c + 512), F.Square, bias=-7.5)
+        mm([(S("A1"), S("Q", 8 - c, 136 - c), S("M", 512 * c, 512 * c + 512))], start=c == 0, stop=c == 7)
+    act(S("qc"), S("A1"))
+    dma(S("meta", 0, 4096, p=slice(0, 128, 16)), S("qc", 0, 512, p=slice(0, 64)), key="meta")
+    dma(S("meta", 0, 4096, p=slice(1, 128, 16)), S("qc", 0, 512, p=slice(64, 128)), key="meta", q="s")
+    act(S("b8"), B8)
+    act(S("b8m"), B8, scale=-1.0 if CFG["MXS"] else -2.0)
+    for f in range(4):
+        act(S("Wd", 8 * f, 8 * f + 8), B8, scale=-1024.0)
+    iota(S("t8", 0, 48), [[-1, 6], [-16, 8]], 0, 1)
+    ts(S("t8", 0, 48), S("t8", 0, 48), 0.0, A.is_equal)
+    row = lambda r: S("t8", 8 * r, 8 * r + 8)
+    tt(row(6), row(0), row(1), A.add)
+    act(row(6), row(6), scale=1024.0)
+    for f in range(4):
+        tt(S("Wm", 8 * f, 8 * f + 8), row(6), row(2 + f), A.add)
+    act(row(7), row(3), scale=64.0)
+    tt(S("Wa", 0, 8), row(2), row(7), A.add)
+    act(S("Wa", 8, 16), S("Wa", 0, 8))
+    act(S("Wa", 16, 24), S("Wa", 0, 8))
+    ts(col(8), lc, 4.0, A.is_equal, -1.0, A.mult)
+    ts(col(9), lc, 5.0, A.is_equal, -64.0, A.mult)
+    act(col(10), col(8), bias=col(9))
+    act(S("Wt"), S("B128"), scale=col(10))
+    act(S("Wl"), S("Wt", 0, 128, 16), scale=-1.0)
+    iota(S("kc", 0, 512, p=p1), [[0, 32], [64, 16]], 0, 0)
+    iota(S("kc", 512, 768, p=p1), [[288, 2], [0, 128]], -255, 0)
+    ms(S("ones"), 1.0)
+    sel(S("Ip"), S("ones"), [[-1, 128]], A.is_equal, 0.0, 0, 1)
+    act(S("In"), S("Ip"), scale=-1.0)
+    act(S("IB"), S("Ip"), scale=8388608.0)
+    act(S("I32"), S("Ip"), scale=32.0)
+    ms(S("rmin"), 0.0)
+    ms(S("rmin", 0, 512, 16), 1.0e9)
+    ts(S("Lb"), S("ic"), -128.0, A.add, lc, A.is_equal)
+    iota(S("mk1"), [[0, 24], [1, 8]], 0, 0)
+    ts(S("mk1"), S("mk1"), bc, A.is_equal)
+    act(S("mk64", 0, 64), S("mk1", 0, 64))
+    act(S("mk64", 64, 128), S("mk1", 0, 64), scale=64.0)
+    act(col(11), hc, scale=5.0)
+    act(S("Y1", 0, 12), S("ic", 0, 12), scale=10.0, bias=col(11))
+    for s in range(1, 4):
+        ts(S("O", 16 * s, 16 * s + 12), S("Y1", 0, 12), float(s), A.add)
+    iota(S("mi"), [[0, 320]], 0, 0)
+    iota(S("pay"), [[0, 320]], 0, 0)
+    for h in range(2):
+        iota(S("pay", 160 * h + 44, 160 * h + 80, 5), [[0, 8]], 32, 0)
+    for nm in ("T", "go", "okk", "Fb", "p34"):
+        iota(S(nm), [[0, T[nm].shape[1]]], 0, 0)
+    sel(S("rs16"), S("ones"), [[0, 8], [1, 16]], A.not_equal, 0.0, 0, 0)
+    sel(S("rsum"), S("ones", 0, 80), [[0, 16], [1, 5]], A.not_equal, 0.0, 0, 0)
+    sel(S("e0"), S("ones", 0, 40), [[0, 8], [1, 5]], A.is_equal, 0.0, 0, 0)
+    iota(S("D128"), [[0, 8], [1, 16]], 0, 0)
+    ts(S("D128"), S("D128"), lc, A.is_equal)
+    act(S("cold", 0, 128), S("ones"), scale=0.5)
+    scan(S("pw"), S("cold", 0, 128), S("Fb", 0, 128), 2.0, A.mult, A.add)
+    tt(S("t128", 0, 16), S("pw", 0, 16), S("D128", 0, 16), A.mult)
+    add("v", lambda e: e.tensor_reduce(T.col[:, 12:13], T.t128[:, 0:16], AxisListType.X, A.add), [S("t128", 0, 16)], [col(12)], 64 * CY)
+    act(S("t128", 128, 256), S("B128"), scale=col(12))
+    for b in range(8):
+        act(S("Wdd", 128 * b, 128 * b + 128), S("t128", 128, 256), scale=2.0 ** (63 - 16 * b))
+    act(S("pw"), S("pw"), scale=2.5 * 2.0 ** 63)
+    tt(S("thr"), S("pw"), S("D128"), A.mult)
+    act(S("Zc", 0, 8), S("ic", 0, 8), scale=16.0, bias=lc)
+    act(S("Zc", 8, 16), S("Zc", 0, 8), scale=-1.0)
+    act(S("Zc", 0, 8), S("Zc", 0, 8), bias=-4096.0)
+    ts(col(13), lc, 2.0, A.not_equal)
+    ts(col(14), lc, 3.0, A.not_equal, col(13), A.mult)
+    act(S("S1m"), S("Ip"), scale=col(14))
+    ts(col(15), col(10), 0.0, A.not_equal)
+    sel(S("c13", 0, 128), S("cold", 0, 128), [[-1, 128]], A.is_equal, 0.0, -2, 1)
+    act(col(16), col(15), scale=2.0)
+    act(S("S2m"), S("c13", 0, 128), scale=col(16))
+    act(col(17), bc, scale=16.0, bias=16.0)
+    ts(col(18), lc, 3.0, A.is_equal, 64.0, A.mult)
+    ts(col(19), lc, 2.0, A.is_equal, col(18), A.add)
+    ts(S("Ya"), S("ic", 0, 144), col(17), A.is_equal, col(19), A.mult)
+    send([(S("z0"), S("z1"), rank + HOP), (S("z0"), S("z2"), rank + 2 * HOP)], "rz", NE)
+    for c in range(8):
+        iota(S("idt", 657 * c, 657 * c + 657), [[1, 657]], 657 * c, 0)
+
+    def conv(h, src, s, nf, mask, groups):
+        ex = S("ex", 192 * h, 192 * h + 64 * nf)
+        tt(ex, IND(src, S("O", 16 * s, 16 * s + 4 * nf)), mask, A.mult)
+        lst = []
+        for q in range(4):
+            lst = []
+            for fs, c0 in groups:
+                for f in fs:
+                    for gi in (2 * q, 2 * q + 1):
+                        o, c = 192 * h + 64 * f + 8 * gi, 128 - 16 * (gi % 2)
+                        lst.append((S("C%d" % h, c0, c0 + 8, p=slice(32 * q, 32 * q + 32)), S("Lb", c, c + 32), S("ex", o, o + 8)))
+            mm(lst)
+
+    def prep(v, h):
+        a, b = 128 * h, 128 * h + 128
+        x, z = S("x%ds" % v, a, b), S("z%d" % v, a, b)
+        Kk, Bk = "K%d" % h, "B%d" % h
+        one = S("ones", 0, 128, p=p1)
+        mm([(S(Kk, 0, 128), S("Wb"), x), (S(Kk, 128, 256), S("Wb"), x),
+            (S(Kk, 0, 128), one, S("kc", 512, 640, p=p1)), (S(Kk, 128, 256), one, S("kc", 640, 768, p=p1))])
+        act(S("Er", a, b), S(Kk, 0, 128), bias=MAGIC)
+        act(S("Er", 256 + a, 256 + b), S("Er", a, b), bias=-MAGIC)
+        tt(S("E", a, b), S(Kk, 128, 256), S("Er", 256 + a, 256 + b), A.subtract)
+        xg = CFG["XG"] if v else 0
+        for k in range(16 - xg):
+            act(S("xr", 16 * a + k, 16 * b, 16), x, bias=-15.0, scale=2.0, key="xr%d" % v)
+        if xg:
+            act(S("mx", a, b), x, bias=-15.0, scale=2.0)
+        for k in range(16 - xg, 16):
+            sel(S("xr", 16 * a + k, 16 * b, 16), S("mx", a, b), [[0, 128]], A.is_ge, 0.0, 0, 0, key="xr%d" % v)
+        mm([(S(Kk, 256, 384), S("Ip"), x), (S(Kk, 256, 384), S("In"), z)])
+        act(S("oz", a, b), S(Kk, 256, 384), F.Abs)
+        if v > 0 and h == 1:
+            mm([(S(Kk, 384, 392), S("ones"), S("good", 8 * j, 8 * j + 8)) for j in range(2 * v)])
+            cp(S("A7"), S(Kk, 384, 392))
+            ts(S("A7"), S("A7"), 7, A.bitwise_and)
+        act(S("C%d" % h, 256, 384), S("E", a, b), bias=-1599.5, scale=48.5)
+        if not CFG["MXS"]:
+            act(S("A%d" % h, 384, 512), z)
+        if CFG["PF"]:
+            act(S(Bk, 0, CFG["PF"]), S("xr", 16 * b - CFG["PF"], 16 * b))
+
+    def step(v, h, s):
+        a, b = 128 * h, 128 * h + 128
+        Kk, Ak, Ck = "K%d" % h, "A%d" % h, "C%d" % h
+        nf = 4 if s == 1 else 2
+        cur = S("cl%d" % v, a, a + 8) if s == 1 else S("cs", 16 * h + 8 * (s - 2), 16 * h + 8 * (s - 2) + 8)
+        tt(S("vi", a, b), IND(S("tm", 128, 1152) if v else S("ti"), cur), S("E", a, b), A.mult)
+        ts(S("ni", a, b), S("vi", a, b), 5, A.arith_shift_right, 4095, A.bitwise_and)
+        cp(S("nu", a, b), S("ni", a, b))
+        t0 = 384 * h
+        act(S("tc", t0 + 128 * (s - 1), t0 + 128 * s), IND(S("meta", 0, 4096), cur))
+        if s == 1:
+            mm([(S(Ck, 64, 72), S("tc", t0, t0 + 128), S("Wl"))])
+            cp(S("pay", 160 * h, 160 * h + 40, 5), S(Ck, 64, 72))
+        o = 2048 * h
+        for c in CFG["CS"]:
+            act(S("M", o, o + c), IND(S("meta", 0, 4096), S("nu", o // 16, (o + c) // 16)), pen=CFG["PENS"])
+            o += c
+        o = 2048 * h
+        for c in CFG["CV"]:
+            tt(S("D", o, o + c), IND(S("pg"), S("nu", o // 16, (o + c) // 16)), S("xr", o, o + c), A.mult, pen=CFG["PEN"])
+            o += c
+        if CFG["PF"]:
+            pf = CFG["PF"]
+            act(S("Pr", 512 * h, 512 * h + pf), IND(S("pg"), S("nu", o // 16, (o + pf) // 16)), pen=CFG["PENP"])
+            for c in range(0, pf, 256):
+                tt(S("D", o + c, o + c + 256), S("Pr", 512 * h + c, 512 * h + c + 256), S("B%d" % h, c, c + 256), A.mult, pen=CFG["PEN"])
+        o = 2048 * h
+        mm([(S(Ak, 128 * j, 128 * j + 128), S("tc", t0 + 128 * j, t0 + 128 * j + 128), S("Wt")) for j in range(s)], stop=False)
+        if CFG["SPA"]:
+            mm([(S(Ak, k, 128 * s, 16, p=slice(0, 96)), S("M", o + k, o + 1536, 16), S("Wa", 0, 8 * s)) for k in range(16)], start=False)
+            mm([(S(Ak, k, 128 * s, 16, p=slice(96, 128)), S("M", o + 1536 + k, o + 2048, 16), S("Wa", 0, 8 * s)) for k in range(16)], start=False)
+        else:
+            mm([(S(Ak, k, 128 * s, 16), S("M", o + k, o + 2048, 16), S("Wa", 0, 8 * s)) for k in range(16)], start=False)
+        if s in CFG["VAR"]:
+            ts(S("bar", t0, t0 + 128 * s), S(Ak, 0, 128 * s), 0.0, A.is_equal)
+        else:
+            act(S("ab", t0, t0 + 128 * s), S(Ak, 0, 128 * s), F.Abs)
+            act(S("bar", t0, t0 + 128 * s), S("ab", t0, t0 + 128 * s), F.Relu, bias=1.0, scale=-1.0)
+        mm([(S(Kk, 0, 128 * nf), S("ones", 0, 128, p=p1), S("kc", 0, 128 * nf, p=p1))], stop=False)
+        mm([(S(Kk, k, 128 * nf, 16), S("M", o + k, o + 2048, 16), S("Wm", 0, 8 * nf)) for k in range(16)], start=False, stop=False)
+        ld = [(S(Kk, k, 128 * nf, 16), S("D", o + k, o + 2048, 16), S("Wd", 0, 8 * nf)) for k in range(16)]
+        lst = []
+        for j in range(s):
+            bj = S("bar", t0 + 128 * j, t0 + 128 * j + 128)
+            lst += [(S(Kk, 128 * f, 128 * f + 128), S("IB"), bj) for f in range(nf)] + [(S(Kk, 128, 256), S("I32"), bj)]
+        if CFG["SPD"]:
+            la = [(S(Kk, k, 128 * nf, 16, p=slice(0, 96)), S("D", o + k, o + 1536, 16), S("Wd", 0, 8 * nf)) for k in range(16)]
+            lb = [(S(Kk, k, 128 * nf, 16, p=slice(96, 128)), S("D", o + 1536 + k, o + 2048, 16), S("Wd", 0, 8 * nf)) for k in range(16)]
+            mm(la + lst + lb if CFG["BARFIRST"] else la + lb + lst, start=False)
+        else:
+            mm(lst + ld if CFG["BARFIRST"] else ld + lst, start=False)
+        c0, p0 = 512 * h, 160 * h
+        scan(S("sc", c0, c0 + 128 * nf), S("rmin", 0, 128 * nf), S(Kk, 0, 128 * nf), 0.0, A.add, A.min)
+        cp(S("mi", p0 + s, p0 + 40 * nf, 5), S("sc", c0 + 15, c0 + 128 * nf, 16))
+        ts(S("pay", p0 + s, p0 + 40 * nf, 5), S("mi", p0 + s, p0 + 40 * nf, 5), 63, A.bitwise_and)
+        if s < 3:
+            conv(h, S("pay", p0, p0 + 80), s, 2, S("mk64"), [((0, 1), 0)])
+            ts(S("cs", 16 * h + 8 * (s - 1), 16 * h + 8 * s), S(Ck, 0, 8), 1023.0, A.min)
+
+    def post(v, h):
+        a, b = 128 * h, 128 * h + 128
+        p0, q0, t0, r0 = 160 * h, 40 * h, 48 * h, 80 * h
+        Ak, Bk, Ck = "A%d" % h, "B%d" % h, "C%d" % h
+        x, z = S("x%ds" % v, a, b), S("z%d" % v, a, b)
+        lst = lambda i: S("lst", 64 * h + 8 * i, 64 * h + 8 * i + 8)
+        ts(S("x1", q0, q0 + 40), S("pay", p0 + 40, p0 + 80), 64.0, A.mult)
+        tt(S("T", t0, t0 + 40), S("pay", p0, p0 + 40), S("x1", q0, q0 + 40), A.add)
+        ts(S("g1", q0, q0 + 40), S("T", t0, t0 + 40), 1024.0, A.is_lt)
+        scan(S("go", t0, t0 + 40), S("g1", q0, q0 + 40), S("e0"), 0.0, A.mult, A.add)
+        tt(S("w", q0, q0 + 40), S("go", t0, t0 + 40), S("go", t0 + 1, t0 + 41), A.subtract)
+        tt(S("p12", r0, r0 + 40), S("w", q0, q0 + 40), S("T", t0, t0 + 40), A.mult)
+        tt(S("p12", r0 + 40, r0 + 80), S("w", q0, q0 + 40), S("T", t0 + 1, t0 + 41), A.mult)
+        scan(S("S1", r0, r0 + 80), S("rsum"), S("p12", r0, r0 + 80), 0.0, A.mult, A.add)
+        conv(h, S("S1", r0, r0 + 80), 3, 2, S("mk1", 0, 128), [((1,), 8), ((0,), 0)])
+        ts(lst(0), S(Ck, 8, 16), -1008.0, A.add, 528.0, A.min)
+        co = S("co%d" % v, a, a + 8)
+        cp(co, S(Ck, 0, 8))
+        xo = S("xo%d" % v, a, b)
+        Kk = "K%d" % h
+        if CFG["TTS"]:
+            act(S("tt", a, b), IND(S("ef"), lst(0)))
+            mm([(S(Kk, 0, 128), S("Ip"), x), (S(Kk, 0, 128), S("In"), S("tt", a, b))])
+            act(xo, S(Kk, 0, 128), F.Abs)
+        else:
+            tt(S("tt", a, b), IND(S("ef"), lst(0)), x, A.subtract)
+            act(xo, S("tt", a, b), F.Abs)
+        if v < NV - 1:
+            send([(xo, S("x%ds" % (v + 1), a, b), rank + HOP), (S("co%d" % v, a, b), S("cl%d" % (v + 1), a, b), rank + HOP)], "r%d%d" % (v, h), NE)
+        else:
+            send([(xo, S("x3s", a, b), rank - HOP * v)], "r%d%d" % (v, h), NE)
+            dma(T.yx[:, a:b], S("x3s", a, b))
+        if CFG["MXS"]:
+            mm([(S(Kk, 128, 256), S("Ip"), xo), (S(Kk, 128, 256), S("In"), z)])
+            act(S("mx", a, b), S(Kk, 128, 256), F.Abs)
+            mm([(S(Ck, 16, 24), S("oz", a, b), S("b8")), (S(Ck, 16, 24), S("mx", a, b), S("b8m"))])
+        else:
+            tt(S("mx", a, b), xo, S(Ak, 384, 512), A.max)
+            mm([(S(Ck, 16, 24), S("oz", a, b), S("b8")), (S(Ck, 16, 24), z, S("b8")), (S(Ck, 16, 24), xo, S("b8")), (S(Ck, 16, 24), S("mx", a, b), S("b8m"))])
+        ts(S("ok", q0, q0 + 40), S("T", t0, t0 + 40), 2048.0, A.is_lt)
+        tt(S("okk", t0 + 1, t0 + 40), S("go", t0, t0 + 39), S("ok", q0 + 1, q0 + 40), A.mult)
+        tt(S("v", q0, q0 + 39), S("okk", t0 + 1, t0 + 40), S("okk", t0 + 2, t0 + 41), A.subtract)
+        ts(S("kk", q0, q0 + 40), S("mi", p0, p0 + 40), 6, A.arith_shift_right, 15, A.bitwise_and)
+        tt(S("p34", r0, r0 + 39), S("kk", q0 + 1, q0 + 40), S("v", q0, q0 + 39), A.mult)
+        tt(S("p34", r0 + 40, r0 + 79), S("T", t0, t0 + 39), S("v", q0, q0 + 39), A.mult)
+        scan(S("Fb", p0 + 80, p0 + 160), S("rsum"), S("p34", r0, r0 + 80), 0.0, A.mult, A.add)
+        pre = lambda i, j=1: S("pre", r0 + 8 * i, r0 + 8 * (i + j))
+        go1, ok1 = S("go", t0 + 1, t0 + 40, 5), S("ok", q0 + 1, q0 + 40, 5)
+        tt(pre(0), S("pay", p0 + 81, p0 + 120, 5), go1, A.mult)
+        act(pre(4), S("Fb", p0 + 123, p0 + 160, 5))
+        tt(pre(2), pre(0), S("Fb", p0 + 123, p0 + 160, 5), A.subtract)
+        ts(pre(1), S("pay", p0 + 121, p0 + 160, 5), 64.0, A.mult, -5248.0, A.add)
+        tt(pre(6), pre(1), go1, A.mult)
+        act(pre(7), ok1, scale=1024.0)
+        tt(pre(3), pre(6), pre(7), A.add)
+        act(pre(5), ok1, scale=-1024.0, bias=5248.0)
+        gd = S("good", 16 * v + 8 * h, 16 * v + 8 * h + 8)
+        if v == 0:
+            ts(gd, S(Ck, 16, 24), 0.0, A.is_gt)
+        else:
+            tt(gd, S(Ck, 16, 24), S("A7"), A.is_gt)
+        tt(pre(8), pre(2), gd, A.mult)
+        tt(pre(9), pre(3), gd, A.mult)
+        tt(S("Fb", p0 + 3, p0 + 80, 5), pre(8, 2), pre(4, 2), A.add)
+        conv(h, S("Fb", p0, p0 + 120), 3, 3, S("mk1"), [((0, 1), 24), ((2,), 32)])
+        key = S(Ck, 24, 32)
+        kl = S("kl", 8 * h, 8 * h + 8)
+        cp(lst(1), key)
+        ts(lst(2), key, -4224.0, A.add, 1023.0, A.min)
+        if v < NV - 1:
+            ts(lst(3), key, 4095.0, A.min)
+        cp(lst(4), S(Ck, 32, 40))
+        act(kl, key)
+        act(S("kcol", a, b), IND(S("idt"), lst(1)))
+        act(S("c13", a, b), IND(S("tm", 128, 1152), lst(2)), scale=13.0)
+        act(S("cold", a, b), IND(S("tm", 128, 1152), lst(2)))
+        act(S(Ak, 0, 128), S("cold", a, b))
+        act(S("Y0", 16 * h, 16 * h + 8), kl, bias=-8192.0)
+        act(S("Y0", 16 * h + 8, 16 * h + 16), kl, bias=4096.0, scale=-1.0)
+        act(S("G2", a, b), IND(S("meta", 0, 4096), co))
+        tt(S("ui", a, b), S("c13", a, b), S(Ck, 256, 384), A.add)
+        ts(S("u2", a, b), S("ui", a, b), 4095, A.bitwise_and)
+        if CFG["DLS"]:
+            act(S("df", a, b), IND(S("D128", 0, 16), lst(4)))
+            tt(S(Ak, 128, 256), S("u2", a, b), S(Ak, 0, 128), A.subtract)
+            tt(S("dl", a, b), S("df", a, b), S(Ak, 128, 256), A.mult)
+        else:
+            tt(S("df", a, b), S("u2", a, b), S(Ak, 0, 128), A.subtract)
+            tt(S("dl", a, b), IND(S("D128", 0, 16), lst(4)), S("df", a, b), A.mult)
+        e0 = 1024 * h
+        for j in range(8):
+            ts(S("eq", e0 + 144 * j, e0 + 128 * j + 128), S("kcol", a + 16 * j, b), S("kl", 8 * h + j, 8 * h + j + 1), A.is_equal)
+        mm([(S(Ck, 128 + 16 * j, 256), S("Wdd", 128 * j, 128 * j + 128), S("eq", e0 + 144 * j, e0 + 128 * j + 128)) for j in range(8)])
+        tt(S("sp", a, b), S(Ck, 128, 256), S("thr"), A.is_lt)
+        scan(S("us", a, b), S("rs16"), S("sp", a, b), 0.0, A.mult, A.add)
+        u = S("us", a + 15, b, 16)
+        tt(S("Y1", 16 * h + 8, 16 * h + 16), S("Y0", 16 * h + 8, 16 * h + 16), u, A.mult)
+        tt(S("Y1", 16 * h, 16 * h + 8), S("Y0", 16 * h, 16 * h + 8), u, A.mult)
+        tt(S("Y0", 16 * h, 16 * h + 16), S("Y1", 16 * h, 16 * h + 16), S("Zc"), A.min)
+        ts(lst(6), S("Y0", 16 * h + 8, 16 * h + 16), -1.0, A.mult)
+        ts(lst(5), S("Y0", 16 * h, 16 * h + 8), 8192.0, A.add)
+        if v < NV - 1:
+            act(S("G1", a, b), IND(S("meta", 0, 4096), lst(3)))
+            mm([(S(Ak, 256, 384), S("S1m"), S("G1", a, b)), (S(Ak, 256, 384), S("S2m"), S("G2", a, b))])
+            act(S("av", a, b), S(Ak, 256, 384))
+        else:
+            mm([(S(Ak, 256, 384), S("Wt"), S("G2", a, b))])
+            act(S("Er", a, b), S(Ak, 256, 384), scale=-1.0)
+
+    for v in range(NV - 1):
+        ms(S("co%d" % v), 0)
+    for v in range(NV):
+        if v == NV - 1:
+            for q in range(4):
+                mm([(S("C0", 256, 512), S("Ya", 16 - j, 144 - j), S("meta", 256 * j, 256 * j + 256)) for j in range(4 * q, 4 * q + 4)],
+                   start=q == 0, stop=q == 3)
+            act(S("t128"), S("C0", 256, 512))
+            dma(S("actf", 0, 4096, p=slice(0, 128, 16)), S("t128"))
+        for h in range(2):
+            early[0] = v == 0 and (h == 1 or CFG["XR0"])
+            prep(v, h)
+        early[0] = False
+        for s in range(1, 4):
+            for h in (1, 0):
+                step(v, h, s)
+        for h in (1, 0):
+            post(v, h)
+        for h in (1, 0):
+            tt(IND(S("tm"), S("lst", 64 * h + 48, 64 * h + 56)), S("dl", 128 * h, 128 * h + 128), S("cold", 128 * h, 128 * h + 128), A.add)
+        for h in (1, 0):
+            off = S("lst", 64 * h + 40, 64 * h + 48)
+            if v < NV - 1:
+                cp(IND(S("meta"), off), S("av", 128 * h, 128 * h + 128))
+            else:
+                cp(IND(S("actf"), off), S("Er", 128 * h, 128 * h + 128))
+    dma(T.yteam[:, 0:512], S("tm", 128, 640), lat=2800.0)
+    dma(T.yteam[:, 512:1024], S("tm", 640, 1152), q="s", lat=2800.0)
+    dma(T.yact[:], S("actf", 0, 4096, p=slice(0, 128, 16)), lat=2300.0)
+    return ops, NE
+
+
+def depends(ops):
+    hist = {}
+    deps = []
+    for i, o in enumerate(ops):
+        d = set()
+        if o["after"] is not None:
+            d.add(o["after"])
+        acc = [(x, False) for x in o["r"]] + [(x, True) for x in o["w"]]
+        for (nm, lo, hi), wr in acc:
+            ps = nm in PSUM
+            for (l2, h2, w2, j) in hist.get(nm, ()):
+                if ps:
+                    if wr or w2 or ops[j]["e"] != o["e"]:
+                        d.add(j)
+                elif (wr or w2) and l2 < hi and lo < h2 and not (o["key"] and o["key"] == ops[j]["key"]):
+                    d.add(j)
+        for (nm, lo, hi), wr in sorted(set(acc)):
+            hs = hist.setdefault(nm, [])
+            if wr and nm in PSUM:
+                hs[:] = [y for y in hs if y[3] == i]
+            hs.append((lo, hi, wr, i))
+        d.discard(i)
+        deps.append(d)
+    anc = []
+    for i, d in enumerate(deps):
+        m = 0
+        for j in d:
+            m |= anc[j]
+        deps[i] = sorted(j for j in d if not m >> j & 1)
+        for j in d:
+            m |= 1 << j
+        anc.append(0 if ops[i]["k"] in "sr" else m)
+    return deps
+
+
+def schedule(ops, deps, order=None):
+    n = len(ops)
+    wake = CFG["WAKE"]
+    pe = [o["e"] == "t" for o in ops]
+    soft = [o["ord"] if CFG["ORD"] and order is None and o["ord"] is not None and o["ord"] not in deps[i] else None for i, o in enumerate(ops)]
+    deps = [d if soft[i] is None else d + [soft[i]] for i, d in enumerate(deps)]
+    succ = [[] for _ in range(n)]
+    for i in range(n):
+        for j in deps[i]:
+            succ[j].append(i)
+
+    def gap(j, i):
+        return 0.0 if soft[i] == j or (pe[i] and pe[j]) else wake + ops[j]["lat"]
+    fin = [0.0] * n
+    st = [0.0] * n
+    free = {}
+    if order is not None:
+        for i in order:
+            e = ops[i]["e"]
+            st[i] = max([free.get(e, 0.0)] + [fin[j] + (-60.0 if pe[i] and pe[j] else wake) for j in deps[i]])
+            free[e] = st[i] + ops[i]["c"]
+            fin[i] = free[e] + ops[i]["lat"]
+        return order, st, fin
+    pr = [0.0] * n
+    for i in range(n - 1, -1, -1):
+        pr[i] = ops[i]["c"] + max([pr[j] + gap(i, j) for j in succ[i]] + [ops[i]["lat"]])
+    r = CFG["SEED"] * 7919 + 1
+    for i in range(n):
+        r = (r * 1103515245 + 12345) % 2147483648
+        pr[i] += CFG["NOISE"] * r / 2147483648.0 - ops[i]["pen"]
+    left = [len(d) for d in deps]
+    rdy = [0.0] * n
+    ready = {}
+    for i in range(n):
+        if not left[i]:
+            ready.setdefault(ops[i]["e"], []).append(i)
+    order = []
+    while len(order) < n:
+        best = None
+        for e, l in ready.items():
+            if not l:
+                continue
+            t = max(free.get(e, 0.0), min(rdy[i] for i in l))
+            if best is None or t < best[0]:
+                best = (t, e)
+        t, e = best
+        i = max((i for i in ready[e] if rdy[i] <= t + CFG["SLACK"].get(e, 40.0)), key=lambda i: (pr[i], -i))
+        ready[e].remove(i)
+        st[i] = max(t, rdy[i])
+        free[e] = st[i] + ops[i]["c"]
+        fin[i] = free[e] + ops[i]["lat"]
+        order.append(i)
+        for j in succ[i]:
+            rdy[j] = max(rdy[j], free[e] + gap(i, j))
+            left[j] -= 1
+            if not left[j]:
+                ready.setdefault(ops[j]["e"], []).append(j)
+
+    def place(seq, pred, fwd):
+        s0 = [0.0] * n
+        lines = {}
+        for i in seq:
+            c = ops[i]["c"]
+            t = 0.0 if fwd else ops[i]["lat"]
+            for j in pred[i]:
+                t = max(t, s0[j] + ops[j]["c"] + (gap(j, i) if fwd else gap(i, j)))
+            ln = lines.setdefault(ops[i]["e"], [])
+            lo, hi = 0, len(ln)
+            while lo < hi:
+                m = (lo + hi) // 2
+                if ln[m][1] <= t:
+                    lo = m + 1
+                else:
+                    hi = m
+            while lo < len(ln) and ln[lo][0] < t + c - 1e-6:
+                t = max(t, ln[lo][1])
+                lo += 1
+            ln.insert(lo, (t, t + c))
+            s0[i] = t
+        return s0
+    best = (max(fin), order, st, fin)
+    for _ in range(CFG["FBI"]):
+        sb = place(sorted(range(n), key=lambda i: (-st[i] - ops[i]["c"], -i)), succ, False)
+        st = place(sorted(range(n), key=lambda i: (-sb[i] - ops[i]["c"], i)), deps, True)
+        fin = [st[i] + ops[i]["c"] + ops[i]["lat"] for i in range(n)]
+        if max(fin) < best[0]:
+            best = (max(fin), sorted(range(n), key=lambda i: (st[i], i)), st, fin)
+    return best[1:]
+
+
+def rank_program(g, core, T, topo):
+    if T.rank_of(core) is None:
+        return
+    ops, NE = build(core, T, topo)
+    if "o" not in _ORDER:
+        deps = depends(ops)
+        _ORDER["d"] = deps
+        _ORDER["o"], _ORDER["st"], _ORDER["fin"] = schedule(ops, deps)
+        _ORDER["ops"] = ops
+    deps, order = _ORDER["d"], _ORDER["o"]
+    eng = {"v": g.vector, "s": g.scalar, "t": g.tensor, "g": g, "y": g.sync}
+    esem = {"v": "sv", "s": "ss", "t": "st", "g": "sg"}
+    n = len(ops)
+    pos = [0] * n
+    for p, i in enumerate(order):
+        pos[i] = p
+    need = [None] * n
+    seen = {e: {} for e in eng}
+    know = [None] * n
+    used = set()
+    for i in order:
+        o = ops[i]
+        if o["k"] == "r":
+            know[i] = {}
+            continue
+        k = seen[o["e"]]
+        w = {}
+        for j in deps[i]:
+            p = ops[j]
+            if p["k"] == "s" or (p["e"] == "t" and o["e"] == "t"):
+                continue
+            s = p["sem"][0] if p["sem"] else esem[p["e"]]
+            if k.get(s, -1) < pos[j] and (s not in w or pos[w[s]] < pos[j]):
+                w[s] = j
+        ws = sorted(w.items(), key=lambda x: -pos[x[1]])
+        need[i] = []
+        for s, j in ws:
+            if k.get(s, -1) < pos[j]:
+                need[i].append((s, j))
+                used.add(j)
+                k[s] = pos[j]
+                for s2, p2 in know[j].items():
+                    if k.get(s2, -1) < p2:
+                        k[s2] = p2
+        know[i] = dict(k)
+    cnt = {}
+    val = [0] * n
+    for i in order:
+        o = ops[i]
+        if o["k"] == "c" and i in used:
+            cnt[o["e"]] = cnt.get(o["e"], 0) + 1
+            val[i] = cnt[o["e"]]
+        elif o["sem"]:
+            val[i] = o["sem"][1]
+    nsend = 0
+    for i in order:
+        o = ops[i]
+        if o["k"] == "r":
+            continue
+        e = eng[o["e"]]
+        for s, j in need[i]:
+            e.wait_ge(T.sem[s], val[j])
+        ins = o["fn"](e)
+        if o["k"] == "d":
+            ins.then_inc(T.sem[o["sem"][0]], 16)
+        elif o["k"] == "s":
+            nsend += 1
+        elif i in used:
+            ins.then_inc(T.sem[esem[o["e"]]], 1)
+    g.wait_ge(T.sem.ls, nsend * NE)
+    for i in order:
+        if ops[i]["k"] in "dr" and i not in used:
+            g.sync.wait_ge(T.sem[ops[i]["sem"][0]], val[i])

@@ -1,14 +1,18 @@
 from concourse.bass import DstId, RemoteDMATransfer
-from concourse.mybir import AluOpType as A, AxisListType, ActivationFunctionType as F
+from concourse.mybir import AluOpType as A, ActivationFunctionType as F
 
 NV, HOP = 3, 3
 CFG = {"GA": 1.56, "SCA": 3.8, "PEC": 0.45, "WAKE": 130.0, "FIX": 0.0, "DM": 1.0,
-       "CV": (512, 256, 256, 256, 256, 256), "CS": (1536, 512), "XG": 10, "PEN": 2000.0, "PENS": 1000.0,
-       "SLACK": {"v": 0.0, "s": 300.0, "t": 0.0}, "SEED": 6, "NOISE": 300.0,
-       "SPD": 0, "SPA": 1, "FBI": 6, "ORD": 1, "PF": 256, "PENP": 3000.0, "MXS": 0, "TTS": 0, "DLS": 1, "XR0": 0, "MM": 4, "VAR": (1,), "BARFIRST": 0,
-       "TOV": ("Wb", "col", "cm", "Wd", "t8", "Wt", "Wl", "In", "IB", "I32", "mk64", "Y1", "Wa", "xr")}
+       "CV": 128, "CS": 256, "CUT": (0, 1536), "XG": 8, "XV": 8, "PEN": 2000.0, "PENS": 1000.0,
+       "SLACK": {"v": 0.0, "s": 0.0, "t": 0.0}, "SEED": 6, "NOISE": 300.0,
+       "SPD": 0, "SPA": 1, "FBI": 6, "ORD": 1, "MM": 4, "VAR": (3,), "UG": 768, "SQ": 8}
 CY = 0.83
 MAGIC = 6442450944.0
+SEG = 19
+KW = 8 * SEG
+SA, ZC, TB, SB, UW = 4096, 4224, 4232, 5256, 5384
+C0, C1 = 1572864.0, 7864320.0
+RR = 16384.0
 
 
 def _scratch():
@@ -16,28 +20,25 @@ def _scratch():
 
     def sb(n, c, d):
         s[n] = ("sbuf", [128, c], d)
-    for n, c in (("pg", 4096), ("meta", 4224), ("D", 4096), ("M", 4096), ("xr", 4096), ("ef", 544), ("cm", 1024), ("qc", 512),
-                 ("Wd", 32), ("Wm", 32), ("Wa", 24), ("Wt", 128), ("Wl", 8), ("kc", 768), ("ones", 128), ("IB", 128),
-                 ("I32", 128), ("Ip", 128), ("In", 128), ("Wb", 128), ("Q", 144), ("Ya", 144), ("Wdd", 1024),
-                 ("S1m", 128), ("S2m", 128), ("rmin", 512), ("rsum", 80), ("rs16", 128), ("e0", 40), ("b8", 8), ("b8m", 8),
-                 ("x0s", 256), ("x1s", 256), ("x2s", 256), ("x3s", 256), ("z0", 256), ("z1", 256), ("z2", 256),
-                 ("xo0", 256), ("xo1", 256), ("xo2", 256), ("tc", 768), ("ab", 768), ("bar", 768), ("Pr", 1024), ("oz", 256),
-                 ("tt", 256), ("mx", 256), ("good", 48), ("eq", 2048), ("sp", 256), ("G1", 256), ("G2", 256), ("av", 256)):
+    for n, c in (("pg", 4096), ("D", 4096), ("M", 4096), ("M1", 4096), ("xr", 4096), ("ef", 544), ("Wd", 16), ("Wm", 16),
+                 ("W3", 144), ("pos", 64), ("npc", 256),
+                 ("Wa", 24), ("Wt", KW), ("kc", 2 * KW), ("ke", 256), ("cst", 48), ("ones", KW), ("Id", 768), ("IW", 136),
+                 ("Wb", 128), ("Q", 144), ("Sel", 1024), ("S2m", 384), ("W1", 144), ("W2", 144), ("dq", 576), ("eq", 1152),
+                 ("es", 1152), ("x0s", 256), ("x1s", 256), ("x2s", 256), ("x3s", 256), ("z0", 256), ("z1", 256), ("z2", 256),
+                 ("xo0", 256), ("xo1", 256), ("xo2", 256), ("tc", 768), ("ab", 6 * KW), ("bar", 6 * KW), ("tt", 256),
+                 ("mx", 256), ("xf", 256), ("G2", 256), ("pay", 128), ("sg", 32), ("kb", 48)):
         sb(n, c, "bfloat16")
-    for n, c in (("Lb", 256), ("ex", 384)):
-        sb(n, c, "float16")
-    for n, c in (("tm", 1160), ("idt", 5256), ("actf", 4224), ("ic", 256), ("R128", 128), ("B128", 128), ("t128", 256),
-                 ("D128", 128), ("mk1", 192), ("mk64", 128), ("col", 24), ("pw", 128), ("thr", 128), ("E", 256), ("Er", 512),
-                 ("sc", 1024), ("T", 96), ("x1", 80), ("g1", 80), ("go", 96), ("w", 80), ("p12", 160), ("S1", 160),
-                 ("ok", 80), ("okk", 96), ("v", 80), ("p34", 160), ("Fb", 320), ("pre", 160), ("kl", 16), ("Y0", 32),
-                 ("Y1", 32), ("Zc", 16), ("kcol", 256), ("us", 256), ("cold", 256), ("c13", 256), ("df", 256), ("dl", 256),
-                 ("t8", 64)):
+    for n, c in (("U", UW), ("idt", 5256), ("ic", 256), ("R", KW), ("Bm", KW), ("B128", 128), ("tmp", 2 * KW), ("D128", 128),
+                 ("col", 40), ("cm", 1280), ("qc", 512), ("E", 256), ("Er", 512), ("rm", 2 * KW), ("sc", 8 * KW),
+                 ("cv", 256), ("cvk", 384), ("VB", 416), ("FL", 320), ("NF", 320), ("c2", 192), ("P", 320), ("RS", 320),
+                 ("SD0", 96), ("SD1", 96), ("SO", 96), ("thr", 16), ("gs", 8), ("gj", 16), ("A7", 1), ("Z", 24), ("spr", 16),
+                 ("y1", 32), ("y2", 16), ("kcol", 256), ("G", 256), ("c13", 256), ("Cb", 512), ("mk", 256), ("dl", 256), ("t8", 80),
+                 ("co0", 128), ("co1", 128), ("Wv0", 512), ("Wv1", 512), ("Wv2", 512)):
         sb(n, c, "float32")
     for n, c in (("ti", 1024), ("ai", 256), ("pi", 512), ("wi", 1), ("si", 16), ("ci", 8), ("vi", 256), ("ni", 256),
-                 ("mi", 320), ("pay", 320), ("kk", 80), ("A7", 8), ("ui", 256), ("u2", 256)):
+                 ("ki", 96), ("Ai", 2), ("ui", 256), ("u2", 256)):
         sb(n, c, "int32")
-    for n, c in (("nu", 256), ("cl0", 256), ("cl1", 256), ("cl2", 256), ("co0", 256), ("co1", 256), ("co2", 256),
-                 ("cs", 32), ("O", 72), ("lst", 128)):
+    for n, c in (("nu", 256), ("cl", 16), ("cs", 64), ("O", 16), ("lst", 192)):
         sb(n, c, "uint16")
     for n in ("K0", "K1", "A0", "A1", "C0", "C1", "B0", "B1"):
         s[n] = ("psum", [128, 512], "float32")
@@ -52,7 +53,7 @@ PSUM = ("K0", "K1", "A0", "A1", "C0", "C1", "B0", "B1")
 _ORDER = {}
 
 
-def build(core, T, topo):
+def build(core, T, topo, cuts):
     rank = T.rank_of(core)
     n = len(T.cores)
     ops = []
@@ -65,6 +66,8 @@ def build(core, T, topo):
         if lo is None:
             lo, hi = 0, t.shape[1]
         ps = slice(None) if p is None else p
+        if step is not None:
+            hi = lo + (hi - 1 - lo) // step * step + 1
         ap = t[ps, lo:hi] if step is None else t[ps, lo:hi:step]
         cnt = (hi - lo + (step or 1) - 1) // (step or 1)
         return (ap, ((name, lo, hi),), cnt, t.dtype)
@@ -100,12 +103,10 @@ def build(core, T, topo):
             return 50 + out[2] * SCA * CY
         return max(64, base) * CY
 
-    def tt(out, a, b, op, pen=0.0):
+    def tt(out, a, b, op, pen=0.0, key=None):
         ps = a[1][0][0] in PSUM or b[1][0][0] in PSUM
         add("v", lambda e: e.tensor_tensor(out[0], a[0], b[0], op), [a, b] + ([out] if out[3] == "ind" else []), [out],
-            vcost(out, a, a[2] * (1 if ps else 2)), pen=pen)
-
-    early = [True]
+            vcost(out, a, a[2] * (1 if ps else 2)), pen=pen, key=key)
 
     def ts(out, a, s1, op0, s2=None, op1=None, key=None):
         c = vcost(out, a, a[2] * (0.5 if two(a) and two(out) else 1))
@@ -114,27 +115,34 @@ def build(core, T, topo):
         else:
             add("v", lambda e: e.tensor_scalar(out[0], a[0], a0(s1), a0(s2), op0, op1), aps([a, s1, s2]), [out], c, key=key)
 
-    def cp(out, a):
-        add("v", lambda e: e.tensor_copy(out[0], a[0]), [a] + ([out] if out[3] == "ind" else []), [out],
-            vcost(out, a, a[2] * (0.5 if two(a) and two(out) else 1)))
+    def cp(out, a, key=None):
+        add("v", lambda e: e.tensor_copy(out[0], a[0]), [a], [out], vcost(out, a, a[2] * (0.5 if two(a) and two(out) else 1)), key=key)
 
-    def ms(out, c):
-        add("v", lambda e: e.memset(out[0], c), [], [out], max(64, out[2] * (0.5 if two(out) else 1)) * CY)
+    def ms(out, c, key=None):
+        add("v", lambda e: e.memset(out[0], c), [], [out], max(64, out[2] * (0.5 if two(out) else 1)) * CY, key=key)
 
-    def scan(out, d0, d1, init, op0, op1):
-        add("v", lambda e: e.tensor_tensor_scan(out[0], d0[0], d1[0], init, op0, op1), [d0, d1], [out], max(64, out[2]) * CY)
+    def scan(out, d0, d1, op0, op1):
+        c = max(64, out[2] * (0.5 if two(out) and two(d0) and two(d1) else 1)) * CY
+        add("v", lambda e: e.tensor_tensor_scan(out[0], d0[0], d1[0], 0.0, op0, op1), [d0, d1], [out], c)
 
-    def act(out, a, f=F.Identity, bias=0.0, scale=1.0, key=None, pen=0.0):
-        if early[0] and f == F.Identity and out[1][0][0] in CFG["TOV"]:
-            return ts(out, a, scale, A.mult, bias, A.add, key=key)
+    def act(out, a, f=F.Identity, bias=0.0, scale=1.0, key=None, pen=0.0, acc=None):
         c = 65 + a[2] * GA * CY if a[3] == "ind" else max(64, a[2]) * CY + 20
-        add("s", lambda e: e.activation(out[0], a[0], f, bias=a0(bias), scale=a0(scale)), aps([a, bias, scale]), [out], c, key=key, pen=pen)
-
-    def iota(out, pat, base, cm):
-        if "int" in str(out[3]):
-            add("g", lambda e: e.iota(out[0], pat, base, cm), [], [out], 130 + 2 * CY * out[2])
+        if acc is None:
+            add("s", lambda e: e.activation(out[0], a[0], f, bias=a0(bias), scale=a0(scale)), aps([a, bias, scale]), [out], c, key=key, pen=pen)
         else:
-            add("g", lambda e: e.iota(out[0], pat, base, cm, allow_small_or_imprecise_dtypes=True), [], [out], 130 + 2 * CY * out[2])
+            add("s", lambda e: e.activation(out[0], a[0], f, bias=a0(bias), scale=a0(scale), accum_out=acc[0]), aps([a, bias, scale]), [out, acc], c + 20)
+
+    def aff(eng, out, a, scale=1.0, bias=0.0, key=None):
+        if eng == "s":
+            act(out, a, bias=bias, scale=scale, key=key)
+        else:
+            ts(out, a, scale, A.mult, bias, A.add, key=key)
+
+    def iota(out, pat, base, cm, key=None):
+        if "int" in str(out[3]):
+            add("g", lambda e: e.iota(out[0], pat, base, cm), [], [out], 130 + 2 * CY * out[2], key=key)
+        else:
+            add("g", lambda e: e.iota(out[0], pat, base, cm, allow_small_or_imprecise_dtypes=True), [], [out], 130 + 2 * CY * out[2], key=key)
 
     def sel(out, a, pat, op, fill, base, cm, key=None):
         add("g", lambda e: e.affine_select(out[0], a[0], pat, op, fill, base, cm), [a], [out], 170 + 2 * CY * out[2], key=key)
@@ -151,7 +159,7 @@ def build(core, T, topo):
                 ins = e.matmul(o[0], l[0], r[0], start and i == 0, stop and i == len(lst) - 1)
             return ins
         add("t", fn, [x[1] for x in lst] + [x[2] for x in lst], [x[0] for x in lst],
-            sum(max(min(64, x[1][2]), x[2][2]) for x in lst) * PEC, lat=60.0)
+            sum(max(min(64, x[1][2]), x[2][2]) * (1 if two(x[1]) else 4) for x in lst) * PEC, lat=60.0)
 
     def dma(out, in_, q="y", key=None, lat=2000.0):
         sem = "d%d" % nd[0]
@@ -178,6 +186,7 @@ def build(core, T, topo):
 
     NE = len(topo.engines(core, T.cores[(rank + HOP) % n]))
     p1 = slice(0, 1)
+    row = lambda r: slice(r, 128, 16)
 
     dma(S("x0s"), T.x0[:])
     dma(S("wi"), T.wt[:], q="s")
@@ -190,359 +199,374 @@ def build(core, T, topo):
     ms(S("ef"), 0.0)
     dma(S("ef", 16, 528), T.eff[:], lat=5800.0)
 
+    ug = CFG["UG"]
+    ms(S("U", 0, 4096 - ug), 1.0)
+    iota(S("U", 4096 - ug, 4096), [[0, ug]], 1, 0)
+    iota(S("U", SA, TB), [[0, TB - SA]], 0, 0)
+    iota(S("U", SB, UW), [[0, UW - SB]], 0, 0)
     iota(S("ci", 0, 1), [[0, 1]], 0, 1)
-    iota(S("R128"), [[-16, 8], [0, 16]], 0, 1)
     iota(S("ic"), [[1, 256]], 0, 0)
-    R8 = S("R128", 0, 128, 16)
-    ms(S("meta", 0, 4096), 0.0)
     ts(S("ci", 1, 2), S("ci", 0, 1), 15, A.bitwise_and)
     ts(S("ci", 2, 3), S("ci", 0, 1), 4, A.arith_shift_right)
     ts(S("ci", 3, 4), S("ci", 0, 1), 3, A.arith_shift_right, 1, A.bitwise_and)
-    cp(S("col", 0, 4), S("ci", 0, 4))
+    ts(S("ci", 4, 5), S("ci", 0, 1), 7, A.bitwise_and)
+    cp(S("col", 0, 5), S("ci", 0, 5))
     col = lambda i: S("col", i, i + 1)
-    pc, lc, bc, hc = col(0), col(1), col(2), col(3)
-    ts(col(4), S("wi"), 2.0, A.mult)
-    ts(S("t128", 0, 128), S("R128"), -0.5, A.is_gt)
-    ts(S("t128", 128, 256), S("R128"), 15.5, A.is_lt)
-    tt(S("B128"), S("t128", 0, 128), S("t128", 128, 256), A.mult)
-    B8 = S("B128", 0, 128, 16)
-    act(S("Wb"), S("B128"), scale=col(4))
-    cp(S("cl0", 0, 8), S("si", 0, 8))
-    cp(S("cl0", 128, 136), S("si", 8, 16))
-    cp(S("tm", 128, 1152), S("ti"))
-    act(col(5), hc, bias=8.0, scale=64.0)
-    act(col(6), bc, bias=col(5), scale=8.0)
-    ts(S("Q"), S("ic", 0, 144), col(6), A.is_equal)
+    lc, bc, hc, l8 = col(1), col(2), col(3), col(4)
     ts(S("pi", 0, 256), S("ai"), 63, A.bitwise_and)
     ts(S("pi", 256, 512), S("ai"), 6, A.arith_shift_right)
     cp(S("cm", 0, 512), S("pi"))
     iota(S("cm", 512, 768), [[0, 4], [1, 64]], 0, 0)
-    iota(S("df"), [[1, 4], [0, 64]], 0, 0)
-    act(col(7), lc, scale=4.0)
-    act(S("cm", 768, 1024), S("df"), bias=col(7))
-    for r in (2, 3, 0, 1):
-        dma(S("meta", 0, 4096, p=slice(2 + r, 128, 16)), S("cm", 256 * r, 256 * r + 256), key="meta")
+    iota(S("dl"), [[1, 4], [0, 64]], 0, 0)
+    aff("s", col(7), lc, 4.0)
+    act(S("cm", 768, 1024), S("dl"), bias=col(7))
+    cp(S("cm", 1024, 1280), S("ai"))
+    for r in (2, 3, 0, 1, 4):
+        dma(S("U", 0, 4096, p=row(2 + r)), S("cm", 256 * r, 256 * r + 256), key="U")
+    aff("v", col(5), hc, 64.0, 8.0)
+    aff("v", col(6), bc, 8.0, col(5))
+    ts(S("Q"), S("ic", 0, 144), col(6), A.is_equal)
     for c in range(8):
         act(S("M", 512 * c, 512 * c + 512), S("pg", 512 * c, 512 * c + 512), F.Square, bias=-7.5)
         mm([(S("A1"), S("Q", 8 - c, 136 - c), S("M", 512 * c, 512 * c + 512))], start=c == 0, stop=c == 7)
     act(S("qc"), S("A1"))
-    dma(S("meta", 0, 4096, p=slice(0, 128, 16)), S("qc", 0, 512, p=slice(0, 64)), key="meta")
-    dma(S("meta", 0, 4096, p=slice(1, 128, 16)), S("qc", 0, 512, p=slice(64, 128)), key="meta", q="s")
-    act(S("b8"), B8)
-    act(S("b8m"), B8, scale=-1.0 if CFG["MXS"] else -2.0)
-    for f in range(4):
-        act(S("Wd", 8 * f, 8 * f + 8), B8, scale=-1024.0)
-    iota(S("t8", 0, 48), [[-1, 6], [-16, 8]], 0, 1)
-    ts(S("t8", 0, 48), S("t8", 0, 48), 0.0, A.is_equal)
-    row = lambda r: S("t8", 8 * r, 8 * r + 8)
-    tt(row(6), row(0), row(1), A.add)
-    act(row(6), row(6), scale=1024.0)
-    for f in range(4):
-        tt(S("Wm", 8 * f, 8 * f + 8), row(6), row(2 + f), A.add)
-    act(row(7), row(3), scale=64.0)
-    tt(S("Wa", 0, 8), row(2), row(7), A.add)
-    act(S("Wa", 8, 16), S("Wa", 0, 8))
-    act(S("Wa", 16, 24), S("Wa", 0, 8))
-    ts(col(8), lc, 4.0, A.is_equal, -1.0, A.mult)
-    ts(col(9), lc, 5.0, A.is_equal, -64.0, A.mult)
-    act(col(10), col(8), bias=col(9))
-    act(S("Wt"), S("B128"), scale=col(10))
-    act(S("Wl"), S("Wt", 0, 128, 16), scale=-1.0)
-    iota(S("kc", 0, 512, p=p1), [[0, 32], [64, 16]], 0, 0)
-    iota(S("kc", 512, 768, p=p1), [[288, 2], [0, 128]], -255, 0)
-    ms(S("ones"), 1.0)
-    sel(S("Ip"), S("ones"), [[-1, 128]], A.is_equal, 0.0, 0, 1)
-    act(S("In"), S("Ip"), scale=-1.0)
-    act(S("IB"), S("Ip"), scale=8388608.0)
-    act(S("I32"), S("Ip"), scale=32.0)
-    ms(S("rmin"), 0.0)
-    ms(S("rmin", 0, 512, 16), 1.0e9)
-    ts(S("Lb"), S("ic"), -128.0, A.add, lc, A.is_equal)
-    iota(S("mk1"), [[0, 24], [1, 8]], 0, 0)
-    ts(S("mk1"), S("mk1"), bc, A.is_equal)
-    act(S("mk64", 0, 64), S("mk1", 0, 64))
-    act(S("mk64", 64, 128), S("mk1", 0, 64), scale=64.0)
-    act(col(11), hc, scale=5.0)
-    act(S("Y1", 0, 12), S("ic", 0, 12), scale=10.0, bias=col(11))
-    for s in range(1, 4):
-        ts(S("O", 16 * s, 16 * s + 12), S("Y1", 0, 12), float(s), A.add)
-    iota(S("mi"), [[0, 320]], 0, 0)
-    iota(S("pay"), [[0, 320]], 0, 0)
-    for h in range(2):
-        iota(S("pay", 160 * h + 44, 160 * h + 80, 5), [[0, 8]], 32, 0)
-    for nm in ("T", "go", "okk", "Fb", "p34"):
-        iota(S(nm), [[0, T[nm].shape[1]]], 0, 0)
-    sel(S("rs16"), S("ones"), [[0, 8], [1, 16]], A.not_equal, 0.0, 0, 0)
-    sel(S("rsum"), S("ones", 0, 80), [[0, 16], [1, 5]], A.not_equal, 0.0, 0, 0)
-    sel(S("e0"), S("ones", 0, 40), [[0, 8], [1, 5]], A.is_equal, 0.0, 0, 0)
+    dma(S("U", 0, 4096, p=row(0)), S("qc", 0, 512, p=slice(0, 64)), key="U")
+    dma(S("U", 0, 4096, p=row(1)), S("qc", 0, 512, p=slice(64, 128)), key="U", q="s")
+
+    def fill(out, c, key=None, p=None):
+        sel(out, S("ic", 0, out[2], p=p), [[0, out[2]]], A.is_gt, c, 0, 0, key=key)
+    iota(S("ones"), [[0, KW]], 1, 0)
+    for nm, w in (("B128", 16), ("Bm", SEG)):
+        sel(S(nm), S("ones", 0, 8 * w), [[-16, 8], [0, w]], A.is_ge, 0.0, 0, 1)
+        sel(S(nm), S(nm), [[16, 8], [0, w]], A.is_ge, 0.0, 15, -1)
+    B8 = S("B128", 0, 128, 16)
+    ts(col(8), S("wi"), 2.0, A.mult)
+    aff("v", S("Wb"), S("B128"), col(8))
+    cp(S("cl"), S("si"))
+    cp(S("U", TB, SB), S("ti"))
+    aff("v", S("Wd", 0, 8), B8, -2048.0)
+    aff("v", S("Wd", 8, 16), B8, -131072.0)
+    ts(col(9), lc, 1.5, A.is_lt, 2048.0, A.mult)
+    for j, (w, r) in enumerate((("Wm", 2), ("Wm", 3))):
+        ts(col(10 + j), lc, float(r), A.is_equal, col(9), A.add)
+        ts(S(w, 8 * (j % 2), 8 * (j % 2) + 8), B8, col(10 + j), A.mult, 64.0 if j % 2 else 1.0, A.mult)
+    ts(col(14), lc, 3.0, A.is_equal, 64.0, A.mult)
+    ts(col(15), lc, 2.0, A.is_equal, col(14), A.add)
+    for j in range(3):
+        aff("v", S("Wa", 8 * j, 8 * j + 8), B8, col(15))
+    ts(col(16), lc, 5.0, A.is_equal, -64.0, A.mult)
+    ts(col(17), lc, 4.0, A.is_equal)
+    tt(col(18), col(16), col(17), A.subtract)
+    ts(col(19), lc, 7.0, A.is_equal)
+    aff("v", S("Wt"), S("Bm"), col(18))
+    for j in (16, 17, 18):
+        aff("v", S("Wt", j, KW, SEG), B8, col(19))
+    sel(S("IW"), S("ones", 0, 136), [[-1, 136]], A.is_equal, 0.0, 2, 1)
+    Ip = S("IW", 2, 130)
+    Id = lambda j: S("Id", 128 * j, 128 * j + 128)
+    for j, c in enumerate((2.0 ** 24, 2.0 ** 30, -C1, -64 * C1, -1024.0)):
+        aff("v", Id(j), Ip, c)
+    iota(S("kc", 0, KW, p=p1), [[0, 8], [128, SEG]], 0, 0)
+    iota(S("kc", KW, 2 * KW, p=p1), [[0, 8], [8192, SEG]], 0, 0)
+    iota(S("rm"), [[0, 2 * KW]], 0, 0)
+    fill(S("rm", 0, 2 * KW, SEG), 2.0 ** 40, key="rm")
+    fill(S("kc", 17, 2 * KW, SEG, p=p1), 2.0 ** 38, key="kc", p=p1)
+    fill(S("kc", 18, 2 * KW, SEG, p=p1), 2.0 ** 38, key="kc", p=p1)
+    for f in range(2):
+        m = 64.0 ** f
+        fill(S("kc", KW * f + 16, KW * f + KW, SEG, p=p1), C0 * m, key="kc", p=p1)
+        fill(S("rm", KW * f + 17, KW * f + KW, SEG), 1.5 * 2.0 ** 30 * m, key="rm")
+        fill(S("rm", KW * f + 18, KW * f + KW, SEG), -1.5 * 2.0 ** 30 * m, key="rm")
+    for j, c in enumerate((C1, 64 * C1, 1024.0, 2048.0)):
+        fill(S("cst", 8 * j, 8 * j + 8, p=p1), c, key="cst", p=p1)
+    iota(S("ke", 0, 256, p=p1), [[288, 2], [0, 128]], -255, 0)
     iota(S("D128"), [[0, 8], [1, 16]], 0, 0)
     ts(S("D128"), S("D128"), lc, A.is_equal)
-    act(S("cold", 0, 128), S("ones"), scale=0.5)
-    scan(S("pw"), S("cold", 0, 128), S("Fb", 0, 128), 2.0, A.mult, A.add)
-    tt(S("t128", 0, 16), S("pw", 0, 16), S("D128", 0, 16), A.mult)
-    add("v", lambda e: e.tensor_reduce(T.col[:, 12:13], T.t128[:, 0:16], AxisListType.X, A.add), [S("t128", 0, 16)], [col(12)], 64 * CY)
-    act(S("t128", 128, 256), S("B128"), scale=col(12))
     for b in range(8):
-        act(S("Wdd", 128 * b, 128 * b + 128), S("t128", 128, 256), scale=2.0 ** (63 - 16 * b))
-    act(S("pw"), S("pw"), scale=2.5 * 2.0 ** 63)
-    tt(S("thr"), S("pw"), S("D128"), A.mult)
-    act(S("Zc", 0, 8), S("ic", 0, 8), scale=16.0, bias=lc)
-    act(S("Zc", 8, 16), S("Zc", 0, 8), scale=-1.0)
-    act(S("Zc", 0, 8), S("Zc", 0, 8), bias=-4096.0)
-    ts(col(13), lc, 2.0, A.not_equal)
-    ts(col(14), lc, 3.0, A.not_equal, col(13), A.mult)
-    act(S("S1m"), S("Ip"), scale=col(14))
-    ts(col(15), col(10), 0.0, A.not_equal)
-    sel(S("c13", 0, 128), S("cold", 0, 128), [[-1, 128]], A.is_equal, 0.0, -2, 1)
-    act(col(16), col(15), scale=2.0)
-    act(S("S2m"), S("c13", 0, 128), scale=col(16))
-    act(col(17), bc, scale=16.0, bias=16.0)
-    ts(col(18), lc, 3.0, A.is_equal, 64.0, A.mult)
-    ts(col(19), lc, 2.0, A.is_equal, col(18), A.add)
-    ts(S("Ya"), S("ic", 0, 144), col(17), A.is_equal, col(19), A.mult)
+        aff("s", S("Sel", 128 * b, 128 * b + 128), S("D128"), S("B128", 16 * b, 16 * b + 1))
+    aff("v", S("O", 0, 1), l8, 8.0, bc)
+    ts(col(20), l8, 3.0, A.add, l8, A.mult)
+    aff("v", S("O", 2, 3), col(20), 8.0, 15.0)
+    lt = lambda lo, hi, st=None: S("tmp", lo, hi, st)
+    iota(lt(0, 40), [[1, 8], [0, 5]], 208, 0)
+    iota(lt(2, 40, 5), [[1, 8]], 224, 0)
+    iota(lt(40, 120), [[0, 2], [8, 8], [64, 5]], 1024 - 128, 0)
+    iota(lt(40, 120, 5), [[0, 2], [1, 8]], 216, 0)
+    iota(lt(41, 120, 5), [[0, 2], [1, 8]], 192, 0)
+    iota(lt(120, 176), [[0, 56]], 0, 0)
+    iota(lt(128, 168), [[24, 8], [8, 5]], 1024 - 8, 0)
+    iota(lt(128, 168, 5), [[0, 8]], 0, 0)
+    iota(lt(132, 168, 5), [[0, 8]], 0, 0)
+    iota(S("P", 0, 176), [[0, 11], [1, 16]], 0, 0)
+    sel(S("NF", 0, 176), S("P", 0, 176), [[0, 11], [1, 16]], A.is_equal, 1.0, 0, 0)
+    ts(S("P", 0, 176), S("P", 0, 176), lc, A.is_equal)
+    tt(S("FL", 0, 176), S("P", 0, 176), lt(0, 176), A.mult)
+    scan(S("RS", 0, 176), S("NF", 0, 176), S("FL", 0, 176), A.mult, A.add)
+    aff("s", col(26), bc, 1.0, -1024.0)
+    ts(S("RS", 176, 187), S("RS", 15, 176, 16), 512.0, A.is_gt, col(26), A.mult)
+    tt(S("RS", 192, 203), S("RS", 176, 187), S("RS", 15, 176, 16), A.add)
+    cp(S("O", 4, 15), S("RS", 192, 203))
+    OA, OE, OW, OK = S("O", 0, 1), S("O", 2, 3), S("O", 4, 12), S("O", 12, 15)
+    aff("v", col(21), bc, 16.0, 15.0)
+    ts(S("W1"), S("ic", 0, 144), col(21), A.is_equal)
+    aff("v", S("W2"), S("W1"), -2.0)
+    aff("v", S("W3"), S("W1"), col(18))
+    iota(S("cvk", 0, 64), [[256, 8], [0, 8]], 0, 0)
+    aff("s", col(25), lc, 16.0)
+    act(S("pos"), S("cvk", 0, 64), bias=col(25))
+    ts(col(22), col(18), 0.0, A.not_equal)
+    aff("s", S("S2m", 0, 128), S("IW", 4, 132), col(22))
+    aff("s", S("S2m", 128, 256), S("IW", 0, 128), col(17))
+    aff("s", col(23), col(16), -1.0)
+    aff("s", S("S2m", 256, 384), S("IW", 1, 129), col(23))
+    aff("s", S("Z", 0, 16), S("D128", 0, 16))
+    ts(col(24), col(15), 0.0, A.not_equal)
+    ts(S("Z", 16, 24), S("ones", 0, 8), lc, A.mult, 6.0, A.is_equal)
+    aff("v", S("Z", 16, 17), S("Z", 17, 18), 1.0, col(24))
+    iota(S("dq"), [[0, 576]], 1, 0)
+    for j in range(8):
+        o = 8 * j * (j + 1)
+        aff("s", S("dq", o + 16 * j, o + 16 * j + 16), S("D128", 0, 16), RR - 1.0, 1.0)
+        iota(S("dq", o, o + 1), [[0, 1]], 0, 0)
+    iota(S("y1", 0, 16), [[0, 2], [16, 8]], 0, 0)
+    act(S("y1", 0, 16), S("y1", 0, 16), bias=lc)
+    aff("s", S("spr"), S("y1", 0, 16), 1.0 / RR, SB / RR)
+    for nm in ("c2", "SD0", "SD1", "co0", "co1"):
+        iota(S(nm), [[0, T[nm].shape[1]]], 0, 0)
+    for h in range(2):
+        iota(S("Wv0", 256 * h + 192, 256 * h + 256), [[0, 64]], 0, 0)
+        for nm, o in (("Wv0", 256 * h + 192), ("co0", 64 * h), ("co1", 64 * h)):
+            aff("s", S(nm, o + 16, o + 24), S("y1", 0, 8), 1.0, float(SA))
+            aff("s", S(nm, o + 24, o + 32), S("y1", 0, 8), 1.0, float(SA - TB))
+        aff("s", S("SD1", 48 * h + 17, 48 * h + 32, 2), S("y1", 0, 8))
+        aff("s", S("SD0", 48 * h + 17, 48 * h + 32, 2), S("y1", 0, 8), 0.0, 128.0)
     send([(S("z0"), S("z1"), rank + HOP), (S("z0"), S("z2"), rank + 2 * HOP)], "rz", NE)
     for c in range(8):
         iota(S("idt", 657 * c, 657 * c + 657), [[1, 657]], 657 * c, 0)
 
-    def conv(h, src, s, nf, mask, groups):
-        ex = S("ex", 192 * h, 192 * h + 64 * nf)
-        tt(ex, IND(src, S("O", 16 * s, 16 * s + 4 * nf)), mask, A.mult)
-        lst = []
-        for q in range(4):
-            lst = []
-            for fs, c0 in groups:
-                for f in fs:
-                    for gi in (2 * q, 2 * q + 1):
-                        o, c = 192 * h + 64 * f + 8 * gi, 128 - 16 * (gi % 2)
-                        lst.append((S("C%d" % h, c0, c0 + 8, p=slice(32 * q, 32 * q + 32)), S("Lb", c, c + 32), S("ex", o, o + 8)))
-            mm(lst)
+    def tolist(out, c0, width, rhs):
+        mm([(S(out, c0 + width * b, c0 + width * b + width), S("Sel", 128 * b, 128 * b + 128), r) for b in range(8) for r in rhs])
+
+    def gain(h, xo, mx):
+        mm([(S("K%d" % h, 0, 8), S(w, 15 - l, 143 - l), S(x[1][0][0], x[1][0][1] + l, x[1][0][2], 16))
+            for w, x in (("W1", xo), ("W2", mx)) for l in range(16)])
 
     def prep(v, h):
         a, b = 128 * h, 128 * h + 128
         x, z = S("x%ds" % v, a, b), S("z%d" % v, a, b)
         Kk, Bk = "K%d" % h, "B%d" % h
         one = S("ones", 0, 128, p=p1)
+        act(S(Bk, 384, 512), z)
+        if v == 0:
+            cp(S("Wv0", 256 * h + 192, 256 * h + 200), S("si", 8 * h, 8 * h + 8))
+        else:
+            cp(S("cl", 8 * h, 8 * h + 8), S("Wv%d" % v, 256 * h + 192, 256 * h + 200))
         mm([(S(Kk, 0, 128), S("Wb"), x), (S(Kk, 128, 256), S("Wb"), x),
-            (S(Kk, 0, 128), one, S("kc", 512, 640, p=p1)), (S(Kk, 128, 256), one, S("kc", 640, 768, p=p1))])
+            (S(Kk, 0, 128), one, S("ke", 0, 128, p=p1)), (S(Kk, 128, 256), one, S("ke", 128, 256, p=p1))])
         act(S("Er", a, b), S(Kk, 0, 128), bias=MAGIC)
         act(S("Er", 256 + a, 256 + b), S("Er", a, b), bias=-MAGIC)
         tt(S("E", a, b), S(Kk, 128, 256), S("Er", 256 + a, 256 + b), A.subtract)
-        xg = CFG["XG"] if v else 0
+        xg, xv = (CFG["XG"], CFG["XV"]) if v else (0, 16 if h else 0)
         for k in range(16 - xg):
-            act(S("xr", 16 * a + k, 16 * b, 16), x, bias=-15.0, scale=2.0, key="xr%d" % v)
+            aff("v" if k < xv else "s", S("xr", 16 * a + k, 16 * b, 16), x, 2.0, -15.0, key="xr%d" % v)
         if xg:
-            act(S("mx", a, b), x, bias=-15.0, scale=2.0)
+            act(S("xf", a, b), x, bias=-15.0, scale=2.0)
         for k in range(16 - xg, 16):
-            sel(S("xr", 16 * a + k, 16 * b, 16), S("mx", a, b), [[0, 128]], A.is_ge, 0.0, 0, 0, key="xr%d" % v)
-        mm([(S(Kk, 256, 384), S("Ip"), x), (S(Kk, 256, 384), S("In"), z)])
-        act(S("oz", a, b), S(Kk, 256, 384), F.Abs)
-        if v > 0 and h == 1:
-            mm([(S(Kk, 384, 392), S("ones"), S("good", 8 * j, 8 * j + 8)) for j in range(2 * v)])
-            cp(S("A7"), S(Kk, 384, 392))
-            ts(S("A7"), S("A7"), 7, A.bitwise_and)
-        act(S("C%d" % h, 256, 384), S("E", a, b), bias=-1599.5, scale=48.5)
-        if not CFG["MXS"]:
-            act(S("A%d" % h, 384, 512), z)
-        if CFG["PF"]:
-            act(S(Bk, 0, CFG["PF"]), S("xr", 16 * b - CFG["PF"], 16 * b))
+            sel(S("xr", 16 * a + k, 16 * b, 16), S("xf", a, b), [[0, 128]], A.is_ge, 0.0, 0, 0, key="xr%d" % v)
+        act(S("Cb", 256 * h, 256 * h + 128), S("E", a, b), bias=-1599.5, scale=48.5)
+
+    def bar_of_success(v, h):
+        a, b = 128 * h, 128 * h + 128
+        thr = S("thr", 8 * h, 8 * h + 8)
+        if v == 0:
+            tt(S("mx", a, b), S("x0s", a, b), S("B%d" % h, 384, 512), A.max)
+            gain(h, S("x0s", a, b), S("mx", a, b))
+            act(thr, S("K%d" % h, 0, 8))
+            return
+        if h == 1:
+            mm([(S("C1", 256, 257), S("B128"), S("gs", j, j + 1)) for j in range(2 * v)])
+            cp(S("Ai", 0, 1), S("C1", 256, 257))
+            ts(S("Ai", 1, 2), S("Ai", 0, 1), 7, A.bitwise_and)
+            cp(S("A7"), S("Ai", 1, 2))
+        act(thr, S("Wv%d" % v, 256 * h + 200, 256 * h + 208), bias=S("A7"))
 
     def step(v, h, s):
         a, b = 128 * h, 128 * h + 128
-        Kk, Ak, Ck = "K%d" % h, "A%d" % h, "C%d" % h
-        nf = 4 if s == 1 else 2
-        cur = S("cl%d" % v, a, a + 8) if s == 1 else S("cs", 16 * h + 8 * (s - 2), 16 * h + 8 * (s - 2) + 8)
-        tt(S("vi", a, b), IND(S("tm", 128, 1152) if v else S("ti"), cur), S("E", a, b), A.mult)
+        Kk, Ak, Bk, Ck = "K%d" % h, "A%d" % h, "B%d" % h, "C%d" % h
+        one = S("ones", 0, 128, p=p1)
+        cur = S("cl", 8 * h, 8 * h + 8) if s == 1 else S("cs", 32 * h + 16 * (s - 2), 32 * h + 16 * (s - 2) + 8)
+        tt(S("vi", a, b), IND(S("U", TB, SB) if v else S("ti"), cur), S("E", a, b), A.mult)
         ts(S("ni", a, b), S("vi", a, b), 5, A.arith_shift_right, 4095, A.bitwise_and)
         cp(S("nu", a, b), S("ni", a, b))
         t0 = 384 * h
-        act(S("tc", t0 + 128 * (s - 1), t0 + 128 * s), IND(S("meta", 0, 4096), cur))
-        if s == 1:
-            mm([(S(Ck, 64, 72), S("tc", t0, t0 + 128), S("Wl"))])
-            cp(S("pay", 160 * h, 160 * h + 40, 5), S(Ck, 64, 72))
+        Mb = "M1" if s == 1 else "M"
+        act(S("tc", t0 + 128 * (s - 1), t0 + 128 * s), IND(S("U", 0, 1024), cur))
         o = 2048 * h
-        for c in CFG["CS"]:
-            act(S("M", o, o + c), IND(S("meta", 0, 4096), S("nu", o // 16, (o + c) // 16)), pen=CFG["PENS"])
+        for c in cuts.get(("s", v, h, s), (CFG["CS"],) * (2048 // CFG["CS"])):
+            act(S(Mb, o, o + c), IND(S("U", 0, 4096), S("nu", o // 16, (o + c) // 16)), pen=CFG["PENS"])
+            ops[-1]["run"] = ("s", v, h, s, o, c)
             o += c
         o = 2048 * h
-        for c in CFG["CV"]:
+        for c in cuts.get(("v", v, h, s), (CFG["CV"],) * (2048 // CFG["CV"])):
             tt(S("D", o, o + c), IND(S("pg"), S("nu", o // 16, (o + c) // 16)), S("xr", o, o + c), A.mult, pen=CFG["PEN"])
+            ops[-1]["run"] = ("v", v, h, s, o, c)
             o += c
-        if CFG["PF"]:
-            pf = CFG["PF"]
-            act(S("Pr", 512 * h, 512 * h + pf), IND(S("pg"), S("nu", o // 16, (o + pf) // 16)), pen=CFG["PENP"])
-            for c in range(0, pf, 256):
-                tt(S("D", o + c, o + c + 256), S("Pr", 512 * h + c, 512 * h + c + 256), S("B%d" % h, c, c + 256), A.mult, pen=CFG["PEN"])
         o = 2048 * h
-        mm([(S(Ak, 128 * j, 128 * j + 128), S("tc", t0 + 128 * j, t0 + 128 * j + 128), S("Wt")) for j in range(s)], stop=False)
-        if CFG["SPA"]:
-            mm([(S(Ak, k, 128 * s, 16, p=slice(0, 96)), S("M", o + k, o + 1536, 16), S("Wa", 0, 8 * s)) for k in range(16)], start=False)
-            mm([(S(Ak, k, 128 * s, 16, p=slice(96, 128)), S("M", o + 1536 + k, o + 2048, 16), S("Wa", 0, 8 * s)) for k in range(16)], start=False)
-        else:
-            mm([(S(Ak, k, 128 * s, 16), S("M", o + k, o + 2048, 16), S("Wa", 0, 8 * s)) for k in range(16)], start=False)
+
+        def sums(bank, w, src, wt, split):
+            if not split:
+                return [(S(bank, k, w, SEG), S(src, o + k, o + 2048, 16), wt) for k in range(16)], []
+            return ([(S(bank, k, w, SEG, p=slice(0, 96)), S(src, o + k, o + 1536, 16), wt) for k in range(16)],
+                    [(S(bank, k, w, SEG, p=slice(96, 128)), S(src, o + 1536 + k, o + 2048, 16), wt) for k in range(16)])
+        mm([(S(Ak, KW * j, KW * j + KW), S("tc", t0 + 128 * j, t0 + 128 * j + 128), S("Wt")) for j in range(s)], stop=False)
+        la, lb = sums(Ak, KW * s, Mb, S("Wa", 0, 8 * s), CFG["SPA"])
+        mm(la, start=False)
+        if lb:
+            mm(lb, start=False)
+        b0 = 3 * KW * h
         if s in CFG["VAR"]:
-            ts(S("bar", t0, t0 + 128 * s), S(Ak, 0, 128 * s), 0.0, A.is_equal)
+            ts(S("bar", b0, b0 + KW * s), S(Ak, 0, KW * s), 0.0, A.is_equal)
         else:
-            act(S("ab", t0, t0 + 128 * s), S(Ak, 0, 128 * s), F.Abs)
-            act(S("bar", t0, t0 + 128 * s), S("ab", t0, t0 + 128 * s), F.Relu, bias=1.0, scale=-1.0)
-        mm([(S(Kk, 0, 128 * nf), S("ones", 0, 128, p=p1), S("kc", 0, 128 * nf, p=p1))], stop=False)
-        mm([(S(Kk, k, 128 * nf, 16), S("M", o + k, o + 2048, 16), S("Wm", 0, 8 * nf)) for k in range(16)], start=False, stop=False)
-        ld = [(S(Kk, k, 128 * nf, 16), S("D", o + k, o + 2048, 16), S("Wd", 0, 8 * nf)) for k in range(16)]
-        lst = []
-        for j in range(s):
-            bj = S("bar", t0 + 128 * j, t0 + 128 * j + 128)
-            lst += [(S(Kk, 128 * f, 128 * f + 128), S("IB"), bj) for f in range(nf)] + [(S(Kk, 128, 256), S("I32"), bj)]
-        if CFG["SPD"]:
-            la = [(S(Kk, k, 128 * nf, 16, p=slice(0, 96)), S("D", o + k, o + 1536, 16), S("Wd", 0, 8 * nf)) for k in range(16)]
-            lb = [(S(Kk, k, 128 * nf, 16, p=slice(96, 128)), S("D", o + 1536 + k, o + 2048, 16), S("Wd", 0, 8 * nf)) for k in range(16)]
-            mm(la + lst + lb if CFG["BARFIRST"] else la + lb + lst, start=False)
+            act(S("ab", b0, b0 + KW * s), S(Ak, 0, KW * s), F.Abs)
+            act(S("bar", b0, b0 + KW * s), S("ab", b0, b0 + KW * s), F.Relu, bias=1.0, scale=-1.0)
+        pay = lambda i: S("pay", 64 * h + 16 * i, 64 * h + 16 * i + 16)
+
+        def keys(bank, wm, carry):
+            mm([(S(bank, 0, 2 * KW), one, S("kc", 0, 2 * KW, p=p1))] + carry, stop=False)
+            mm(sums(bank, 2 * KW, Mb, S(wm), 0)[0], start=False, stop=False)
+            lst = [(S(bank, KW * f, KW * f + KW), Id(f), S("bar", b0 + KW * j, b0 + KW * j + KW)) for j in range(s) for f in range(2)]
+            la, lb = sums(bank, 2 * KW, "D", S("Wd"), CFG["SPD"] and bank == Kk)
+            mm(la, start=False, stop=False)
+            mm(lst, start=False)
+            if lb:
+                mm(lb, start=False)
+        both, hi = S(Kk, 16, 2 * KW, SEG), S(Kk, KW + 16, 2 * KW, SEG)
+        if s == 1:
+            carry = [(both, one, S("cst", 0, 16, p=p1)), (hi, one, S("cst", 24, 32, p=p1))]
         else:
-            mm(lst + ld if CFG["BARFIRST"] else ld + lst, start=False)
-        c0, p0 = 512 * h, 160 * h
-        scan(S("sc", c0, c0 + 128 * nf), S("rmin", 0, 128 * nf), S(Kk, 0, 128 * nf), 0.0, A.add, A.min)
-        cp(S("mi", p0 + s, p0 + 40 * nf, 5), S("sc", c0 + 15, c0 + 128 * nf, 16))
-        ts(S("pay", p0 + s, p0 + 40 * nf, 5), S("mi", p0 + s, p0 + 40 * nf, 5), 63, A.bitwise_and)
+            sg = S("sg", 16 * h + 8 * (s - 2), 16 * h + 8 * (s - 2) + 8)
+            carry = [(hi, one, S("cst", 16, 24, p=p1)), (both, Ip, pay(s - 1)), (S(Kk, 16, KW, SEG), Id(2), sg), (hi, Id(3), sg), (hi, Id(4), sg)]
+        keys(Kk, "Wm", carry)
+        c0 = 4 * KW * h + KW * (s - 1)
+        scan(S("sc", c0, c0 + 2 * KW), S("rm"), S(Kk, 0, 2 * KW), A.add, A.min)
+        tt(pay(s), S("sc", c0 + 16, c0 + 2 * KW, SEG), S("sc", c0 + 18, c0 + 2 * KW, SEG), A.subtract)
+        p0 = 64 * h + 16 * s
+        tolist(Ck, 0, 8, [S("pay", p0, p0 + 8), S("pay", p0 + 8, p0 + 16)])
+        cva = S("Wv%d" % v, 256 * h + 64 * (s - 1), 256 * h + 64 * s)
+        act(cva, S(Ck, 0, 64))
         if s < 3:
-            conv(h, S("pay", p0, p0 + 80), s, 2, S("mk64"), [((0, 1), 0)])
-            ts(S("cs", 16 * h + 8 * (s - 1), 16 * h + 8 * s), S(Ck, 0, 8), 1023.0, A.min)
+            ts(S("cs", 32 * h + 16 * (s - 1), 32 * h + 16 * s), IND(cva, OA), 1023.0, A.min)
+            act(S("sg", 16 * h + 8 * (s - 1), 16 * h + 8 * s), S("pay", p0 + 8, p0 + 16), F.Sign, bias=-1000.0)
+        else:
+            ts(S("lst", 96 * h, 96 * h + 16), IND(cva, OA), -1008.0, A.add, 528.0, A.min)
+        if s == 1:
+            q = 48 * h
+            cp(S("ki", q, q + 8), S("sc", c0 + 18, c0 + KW, SEG))
+            ts(S("ki", q + 24, q + 32), S("ki", q, q + 8), 7, A.arith_shift_right, 15, A.bitwise_and)
+            cp(S("kb", 24 * h, 24 * h + 8), S("ki", q + 24, q + 32))
+            mm([(S(Bk, 0, 64), Ip, S("pos"))], stop=False)
+            mm([(S(Bk, 8 * j, 8 * j + 8), S("Sel", 128 * j, 128 * j + 128), S("kb", 24 * h, 24 * h + 8)) for j in range(8)], start=False)
+            act(S("cv", a, a + 64), S(Bk, 0, 64))
+            cp(S("lst", 96 * h + 80, 96 * h + 96), IND(S("cv", a, a + 64), OA))
+            act(S("npc", a, b), IND(S("M1", o, o + 2048), S("lst", 96 * h + 80, 96 * h + 88)))
+            mm([(S(Bk, 64, 72), S("W3", 15 - l, 143 - l), S("npc", a + l, b, 16)) for l in range(16)])
+            act(S("Wv%d" % v, 256 * h + 224, 256 * h + 232), S(Bk, 64, 72), scale=-1.0)
 
     def post(v, h):
         a, b = 128 * h, 128 * h + 128
-        p0, q0, t0, r0 = 160 * h, 40 * h, 48 * h, 80 * h
-        Ak, Bk, Ck = "A%d" % h, "B%d" % h, "C%d" % h
-        x, z = S("x%ds" % v, a, b), S("z%d" % v, a, b)
-        lst = lambda i: S("lst", 64 * h + 8 * i, 64 * h + 8 * i + 8)
-        ts(S("x1", q0, q0 + 40), S("pay", p0 + 40, p0 + 80), 64.0, A.mult)
-        tt(S("T", t0, t0 + 40), S("pay", p0, p0 + 40), S("x1", q0, q0 + 40), A.add)
-        ts(S("g1", q0, q0 + 40), S("T", t0, t0 + 40), 1024.0, A.is_lt)
-        scan(S("go", t0, t0 + 40), S("g1", q0, q0 + 40), S("e0"), 0.0, A.mult, A.add)
-        tt(S("w", q0, q0 + 40), S("go", t0, t0 + 40), S("go", t0 + 1, t0 + 41), A.subtract)
-        tt(S("p12", r0, r0 + 40), S("w", q0, q0 + 40), S("T", t0, t0 + 40), A.mult)
-        tt(S("p12", r0 + 40, r0 + 80), S("w", q0, q0 + 40), S("T", t0 + 1, t0 + 41), A.mult)
-        scan(S("S1", r0, r0 + 80), S("rsum"), S("p12", r0, r0 + 80), 0.0, A.mult, A.add)
-        conv(h, S("S1", r0, r0 + 80), 3, 2, S("mk1", 0, 128), [((1,), 8), ((0,), 0)])
-        ts(lst(0), S(Ck, 8, 16), -1008.0, A.add, 528.0, A.min)
-        co = S("co%d" % v, a, a + 8)
-        cp(co, S(Ck, 0, 8))
+        Kk, Ak, Bk, Ck = "K%d" % h, "A%d" % h, "B%d" % h, "C%d" % h
+        x = S("x%ds" % v, a, b)
+        lst = lambda i, j=1: S("lst", 96 * h + 8 * i, 96 * h + 8 * (i + j))
+        v0, f0, s0 = 208 * h, 160 * h, 48 * h
         xo = S("xo%d" % v, a, b)
-        Kk = "K%d" % h
-        if CFG["TTS"]:
-            act(S("tt", a, b), IND(S("ef"), lst(0)))
-            mm([(S(Kk, 0, 128), S("Ip"), x), (S(Kk, 0, 128), S("In"), S("tt", a, b))])
-            act(xo, S(Kk, 0, 128), F.Abs)
-        else:
-            tt(S("tt", a, b), IND(S("ef"), lst(0)), x, A.subtract)
-            act(xo, S("tt", a, b), F.Abs)
+        tt(S("tt", a, b), IND(S("ef"), lst(0)), x, A.subtract)
+        act(xo, S("tt", a, b), F.Abs)
+        tt(S("mx", a, b), xo, S(Bk, 384, 512), A.max)
+        gain(h, xo, S("mx", a, b))
+        thr = S("thr", 8 * h, 8 * h + 8)
+        tt(S("SD1", s0, s0 + 16, 2), S(Kk, 0, 8), thr, A.is_gt, key="g%d%d" % (v, h))
+        cp(S("ki", s0 + 8, s0 + 24), S("sc", 4 * KW * h + KW + 18, 4 * KW * h + 3 * KW, SEG))
+        ts(S("ki", s0 + 32, s0 + 48), S("ki", s0 + 8, s0 + 24), 7, A.arith_shift_right, 15, A.bitwise_and)
+        cp(S("kb", 24 * h + 8, 24 * h + 24), S("ki", s0 + 32, s0 + 48))
+        tolist(Ak, 0, 24, [S("kb", 24 * h, 24 * h + 24)])
+        act(S("cvk", 192 * h, 192 * h + 192), S(Ak, 0, 192))
+        act(S("VB", v0 + 128, v0 + 176), IND(S("cvk", 192 * h, 192 * h + 192), OK))
+        act(S("VB", v0, v0 + 128), IND(S("Wv%d" % v, 256 * h, 256 * h + 256), OW))
+        ts(S("FL", f0, f0 + 80), S("VB", v0 + 40, v0 + 120), 1024.0, A.is_lt)
+        ts(S("c2", 96 * h, 96 * h + 80), S("VB", v0 + 40, v0 + 120), 2048.0, A.is_lt)
+        tt(S("FL", f0 + 80, f0 + 160), S("FL", f0, f0 + 80), S("c2", 96 * h + 1, 96 * h + 81), A.mult)
+        act(S("NF", f0, f0 + 160), S("FL", f0, f0 + 160), bias=1.0, scale=-1.0)
+        tt(S("P", f0, f0 + 120), S("FL", f0, f0 + 120), S("VB", v0, v0 + 120), A.mult)
+        scan(S("RS", f0, f0 + 120), S("NF", f0, f0 + 120), S("P", f0, f0 + 120), A.mult, A.add)
+        tt(S("P", f0 + 120, f0 + 160), S("FL", f0 + 120, f0 + 160), S("VB", v0 + 128, v0 + 168), A.mult)
+        scan(S("RS", f0 + 120, f0 + 160), S("NF", f0 + 120, f0 + 160), S("P", f0 + 120, f0 + 160), A.mult, A.add)
+        kg, L, kf, ks = S("RS", f0 + 2, f0 + 40, 5), S("RS", f0 + 44, f0 + 80, 5), S("RS", f0 + 83, f0 + 120, 5), S("RS", f0 + 123, f0 + 160, 5)
+        kfo = S("SD1", s0 + 1, s0 + 16, 2)
+        act(kfo, kf, bias=float(TB), key="g%d%d" % (v, h))
+        tt(S("SD0", s0 + 1, s0 + 16, 2), kg, kfo, A.subtract)
+        cp(lst(2), L)
         if v < NV - 1:
-            send([(xo, S("x%ds" % (v + 1), a, b), rank + HOP), (S("co%d" % v, a, b), S("cl%d" % (v + 1), a, b), rank + HOP)], "r%d%d" % (v, h), NE)
+            co = "co%d" % v
+            act(S(co, 64 * h, 64 * h + 8), L)
+            act(S(co, 64 * h + 8, 64 * h + 16), S(Kk, 0, 8))
+            send([(xo, S("x%ds" % (v + 1), a, b), rank + HOP), (S(co, 64 * h, 64 * h + 64), S("Wv%d" % (v + 1), 256 * h + 192, 256 * h + 256), rank + HOP)],
+                 "r%d%d" % (v, h), NE)
         else:
             send([(xo, S("x3s", a, b), rank - HOP * v)], "r%d%d" % (v, h), NE)
             dma(T.yx[:, a:b], S("x3s", a, b))
-        if CFG["MXS"]:
-            mm([(S(Kk, 128, 256), S("Ip"), xo), (S(Kk, 128, 256), S("In"), z)])
-            act(S("mx", a, b), S(Kk, 128, 256), F.Abs)
-            mm([(S(Ck, 16, 24), S("oz", a, b), S("b8")), (S(Ck, 16, 24), S("mx", a, b), S("b8m"))])
-        else:
-            tt(S("mx", a, b), xo, S(Ak, 384, 512), A.max)
-            mm([(S(Ck, 16, 24), S("oz", a, b), S("b8")), (S(Ck, 16, 24), z, S("b8")), (S(Ck, 16, 24), xo, S("b8")), (S(Ck, 16, 24), S("mx", a, b), S("b8m"))])
-        ts(S("ok", q0, q0 + 40), S("T", t0, t0 + 40), 2048.0, A.is_lt)
-        tt(S("okk", t0 + 1, t0 + 40), S("go", t0, t0 + 39), S("ok", q0 + 1, q0 + 40), A.mult)
-        tt(S("v", q0, q0 + 39), S("okk", t0 + 1, t0 + 40), S("okk", t0 + 2, t0 + 41), A.subtract)
-        ts(S("kk", q0, q0 + 40), S("mi", p0, p0 + 40), 6, A.arith_shift_right, 15, A.bitwise_and)
-        tt(S("p34", r0, r0 + 39), S("kk", q0 + 1, q0 + 40), S("v", q0, q0 + 39), A.mult)
-        tt(S("p34", r0 + 40, r0 + 79), S("T", t0, t0 + 39), S("v", q0, q0 + 39), A.mult)
-        scan(S("Fb", p0 + 80, p0 + 160), S("rsum"), S("p34", r0, r0 + 80), 0.0, A.mult, A.add)
-        pre = lambda i, j=1: S("pre", r0 + 8 * i, r0 + 8 * (i + j))
-        go1, ok1 = S("go", t0 + 1, t0 + 40, 5), S("ok", q0 + 1, q0 + 40, 5)
-        tt(pre(0), S("pay", p0 + 81, p0 + 120, 5), go1, A.mult)
-        act(pre(4), S("Fb", p0 + 123, p0 + 160, 5))
-        tt(pre(2), pre(0), S("Fb", p0 + 123, p0 + 160, 5), A.subtract)
-        ts(pre(1), S("pay", p0 + 121, p0 + 160, 5), 64.0, A.mult, -5248.0, A.add)
-        tt(pre(6), pre(1), go1, A.mult)
-        act(pre(7), ok1, scale=1024.0)
-        tt(pre(3), pre(6), pre(7), A.add)
-        act(pre(5), ok1, scale=-1024.0, bias=5248.0)
-        gd = S("good", 16 * v + 8 * h, 16 * v + 8 * h + 8)
-        if v == 0:
-            ts(gd, S(Ck, 16, 24), 0.0, A.is_gt)
-        else:
-            tt(gd, S(Ck, 16, 24), S("A7"), A.is_gt)
-        tt(pre(8), pre(2), gd, A.mult)
-        tt(pre(9), pre(3), gd, A.mult)
-        tt(S("Fb", p0 + 3, p0 + 80, 5), pre(8, 2), pre(4, 2), A.add)
-        conv(h, S("Fb", p0, p0 + 120), 3, 3, S("mk1"), [((0, 1), 24), ((2,), 32)])
-        key = S(Ck, 24, 32)
-        kl = S("kl", 8 * h, 8 * h + 8)
-        cp(lst(1), key)
-        ts(lst(2), key, -4224.0, A.add, 1023.0, A.min)
-        if v < NV - 1:
-            ts(lst(3), key, 4095.0, A.min)
-        cp(lst(4), S(Ck, 32, 40))
-        act(kl, key)
-        act(S("kcol", a, b), IND(S("idt"), lst(1)))
-        act(S("c13", a, b), IND(S("tm", 128, 1152), lst(2)), scale=13.0)
-        act(S("cold", a, b), IND(S("tm", 128, 1152), lst(2)))
-        act(S(Ak, 0, 128), S("cold", a, b))
-        act(S("Y0", 16 * h, 16 * h + 8), kl, bias=-8192.0)
-        act(S("Y0", 16 * h + 8, 16 * h + 16), kl, bias=4096.0, scale=-1.0)
-        act(S("G2", a, b), IND(S("meta", 0, 4096), co))
-        tt(S("ui", a, b), S("c13", a, b), S(Ck, 256, 384), A.add)
-        ts(S("u2", a, b), S("ui", a, b), 4095, A.bitwise_and)
-        if CFG["DLS"]:
-            act(S("df", a, b), IND(S("D128", 0, 16), lst(4)))
-            tt(S(Ak, 128, 256), S("u2", a, b), S(Ak, 0, 128), A.subtract)
-            tt(S("dl", a, b), S("df", a, b), S(Ak, 128, 256), A.mult)
-        else:
-            tt(S("df", a, b), S("u2", a, b), S(Ak, 0, 128), A.subtract)
-            tt(S("dl", a, b), IND(S("D128", 0, 16), lst(4)), S("df", a, b), A.mult)
-        e0 = 1024 * h
+        scan(S("SO", s0, s0 + 16), S("SD0", s0, s0 + 16), S("SD1", s0, s0 + 16), A.mult, A.add)
+        key = S("SO", s0 + 1, s0 + 16, 2)
+        cp(lst(3), key)
+        act(S("kcol", a, b), IND(S("idt"), lst(3)))
+        e0 = 576 * h
         for j in range(8):
-            ts(S("eq", e0 + 144 * j, e0 + 128 * j + 128), S("kcol", a + 16 * j, b), S("kl", 8 * h + j, 8 * h + j + 1), A.is_equal)
-        mm([(S(Ck, 128 + 16 * j, 256), S("Wdd", 128 * j, 128 * j + 128), S("eq", e0 + 144 * j, e0 + 128 * j + 128)) for j in range(8)])
-        tt(S("sp", a, b), S(Ck, 128, 256), S("thr"), A.is_lt)
-        scan(S("us", a, b), S("rs16"), S("sp", a, b), 0.0, A.mult, A.add)
-        u = S("us", a + 15, b, 16)
-        tt(S("Y1", 16 * h + 8, 16 * h + 16), S("Y0", 16 * h + 8, 16 * h + 16), u, A.mult)
-        tt(S("Y1", 16 * h, 16 * h + 8), S("Y0", 16 * h, 16 * h + 8), u, A.mult)
-        tt(S("Y0", 16 * h, 16 * h + 16), S("Y1", 16 * h, 16 * h + 16), S("Zc"), A.min)
-        ts(lst(6), S("Y0", 16 * h + 8, 16 * h + 16), -1.0, A.mult)
-        ts(lst(5), S("Y0", 16 * h, 16 * h + 8), 8192.0, A.add)
+            o = e0 + 8 * j * (j + 1)
+            ts(S("eq", o, o + 16 * j + 16), S("kcol", a, a + 16 * j + 16), S("SO", s0 + 2 * j + 1, s0 + 2 * j + 2), A.is_equal)
+        scan(S("es", e0, e0 + 576), S("dq"), S("eq", e0, e0 + 576), A.mult, A.max)
+        tt(S("y1", 16 * h, 16 * h + 16), IND(S("es", e0, e0 + 576), OE), S("spr"), A.mult)
+        tt(S("y2", 8 * h, 8 * h + 8), S("y1", 16 * h, 16 * h + 8), key, A.max)
+        cp(lst(4), S("y2", 8 * h, 8 * h + 8))
+        ts(lst(5), key, float(ZC), A.max)
+        gd = S("SD1", s0, s0 + 16, 2)
         if v < NV - 1:
-            act(S("G1", a, b), IND(S("meta", 0, 4096), lst(3)))
-            mm([(S(Ak, 256, 384), S("S1m"), S("G1", a, b)), (S(Ak, 256, 384), S("S2m"), S("G2", a, b))])
-            act(S("av", a, b), S(Ak, 256, 384))
+            act(S("SD1", s0 + 16, s0 + 32, 2), gd, acc=S("gs", 2 * v + h, 2 * v + h + 1))
         else:
-            mm([(S(Ak, 256, 384), S("Wt"), S("G2", a, b))])
-            act(S("Er", a, b), S(Ak, 256, 384), scale=-1.0)
+            act(S("SD1", s0 + 16, s0 + 32, 2), gd)
+        act(S("SD1", s0 + 32, s0 + 48, 2), gd)
+        act(S("SD1", s0 + 33, s0 + 48, 2), ks)
+        act(S("SD0", s0 + 33, s0 + 48, 2), ks, bias=16.0, scale=-1.0)
+        scan(S("SO", s0 + 16, s0 + 48), S("SD0", s0 + 16, s0 + 48), S("SD1", s0 + 16, s0 + 48), A.mult, A.add)
+        cp(lst(6, 2), S("SO", s0 + 17, s0 + 48, 2))
+        act(S("G2", a, b), IND(S("U", 0, 1024), lst(2)))
+        mm([(S(Ck, 128, 256), S("S2m", 128 * j, 128 * j + 128), S("G2", a, b)) for j in range(3)])
+        act(S("Cb", 256 * h + 128, 256 * h + 256), S(Ck, 128, 256))
+        act(S("c13", a, b), IND(S("U", 0, SB), lst(5)), scale=13.0)
+        act(S("G", a, b), IND(S("U", 0, SB), lst(3)))
+        act(S(Bk, 0, 128), S("G", a, b))
+        act(S("mk", a, b), IND(S("Z"), lst(7)))
+        tt(S("ui", a, b), IND(S("Cb", 256 * h, 256 * h + 256), lst(6)), S("c13", a, b), A.add)
+        ts(S("u2", a, b), S("ui", a, b), 4095, A.bitwise_and)
+        tt(S(Ak, 256, 384), S("u2", a, b), S(Bk, 0, 128), A.subtract)
+        tt(S("dl", a, b), S("mk", a, b), S(Ak, 256, 384), A.mult)
 
-    for v in range(NV - 1):
-        ms(S("co%d" % v), 0)
     for v in range(NV):
-        if v == NV - 1:
-            for q in range(4):
-                mm([(S("C0", 256, 512), S("Ya", 16 - j, 144 - j), S("meta", 256 * j, 256 * j + 256)) for j in range(4 * q, 4 * q + 4)],
-                   start=q == 0, stop=q == 3)
-            act(S("t128"), S("C0", 256, 512))
-            dma(S("actf", 0, 4096, p=slice(0, 128, 16)), S("t128"))
-        for h in range(2):
-            early[0] = v == 0 and (h == 1 or CFG["XR0"])
+        for h in (1, 0):
             prep(v, h)
-        early[0] = False
+        for h in (1, 0):
+            if v == 0:
+                bar_of_success(v, h)
         for s in range(1, 4):
             for h in (1, 0):
                 step(v, h, s)
+                if v and s == 1:
+                    bar_of_success(v, h)
         for h in (1, 0):
             post(v, h)
         for h in (1, 0):
-            tt(IND(S("tm"), S("lst", 64 * h + 48, 64 * h + 56)), S("dl", 128 * h, 128 * h + 128), S("cold", 128 * h, 128 * h + 128), A.add)
-        for h in (1, 0):
-            off = S("lst", 64 * h + 40, 64 * h + 48)
-            if v < NV - 1:
-                cp(IND(S("meta"), off), S("av", 128 * h, 128 * h + 128))
-            else:
-                cp(IND(S("actf"), off), S("Er", 128 * h, 128 * h + 128))
-    dma(T.yteam[:, 0:512], S("tm", 128, 640), lat=2800.0)
-    dma(T.yteam[:, 512:1024], S("tm", 640, 1152), q="s", lat=2800.0)
-    dma(T.yact[:], S("actf", 0, 4096, p=slice(0, 128, 16)), lat=2300.0)
+            tt(IND(S("U"), S("lst", 96 * h + 32, 96 * h + 40)), S("dl", 128 * h, 128 * h + 128), S("G", 128 * h, 128 * h + 128), A.add)
+    dma(T.yteam[:, 0:512], S("U", TB, TB + 512), lat=2800.0)
+    dma(T.yteam[:, 512:1024], S("U", TB + 512, SB), q="s", lat=2800.0)
+    dma(T.yact[:], S("U", 0, 4096, p=row(6)), lat=2300.0)
     return ops, NE
 
 
@@ -581,7 +605,7 @@ def depends(ops):
     return deps
 
 
-def schedule(ops, deps, order=None):
+def schedule(ops, deps, order=None, first=None, fbi=0):
     n = len(ops)
     wake = CFG["WAKE"]
     pe = [o["e"] == "t" for o in ops]
@@ -618,6 +642,9 @@ def schedule(ops, deps, order=None):
         if not left[i]:
             ready.setdefault(ops[i]["e"], []).append(i)
     order = []
+    prev = {}
+    if first is not None:
+        order, st, fin = schedule(ops, deps, first)
     while len(order) < n:
         best = None
         for e, l in ready.items():
@@ -630,6 +657,11 @@ def schedule(ops, deps, order=None):
         i = max((i for i in ready[e] if rdy[i] <= t + CFG["SLACK"].get(e, 40.0)), key=lambda i: (pr[i], -i))
         ready[e].remove(i)
         st[i] = max(t, rdy[i])
+        ru = ops[i].get("run")
+        if ru and prev.get(e) == ops[i]["ord"] and ru[4] % 2048 not in CFG["CUT"] and st[i] <= free[e] + 1.0:
+            ops[i]["c"] -= 50.0 if e == "v" else 65.0
+            ops[i]["join"] = True
+        prev[e] = i
         free[e] = st[i] + ops[i]["c"]
         fin[i] = free[e] + ops[i]["lat"]
         order.append(i)
@@ -662,7 +694,7 @@ def schedule(ops, deps, order=None):
             s0[i] = t
         return s0
     best = (max(fin), order, st, fin)
-    for _ in range(CFG["FBI"]):
+    for _ in range(fbi):
         sb = place(sorted(range(n), key=lambda i: (-st[i] - ops[i]["c"], -i)), succ, False)
         st = place(sorted(range(n), key=lambda i: (-sb[i] - ops[i]["c"], i)), deps, True)
         fin = [st[i] + ops[i]["c"] + ops[i]["lat"] for i in range(n)]
@@ -671,15 +703,31 @@ def schedule(ops, deps, order=None):
     return best[1:]
 
 
+def plan(core, T, topo):
+    ops, _ = build(core, T, topo, {})
+    order, st, fin = schedule(ops, depends(ops), fbi=0)
+    cuts, head, kept = {}, {}, []
+    for i, o in enumerate(ops):
+        ru = o.get("run")
+        if ru and o.get("join"):
+            cuts[ru[:4]][-1] += ru[5]
+            continue
+        if ru:
+            cuts.setdefault(ru[:4], []).append(ru[5])
+        head[i] = len(kept)
+        kept.append(i)
+    ops, _ = build(core, T, topo, cuts)
+    deps = depends(ops)
+    order, st, fin = schedule(ops, deps, first=[head[i] for i in order if i in head], fbi=CFG["FBI"])
+    return cuts, deps, order, st, fin
+
+
 def rank_program(g, core, T, topo):
     if T.rank_of(core) is None:
         return
-    ops, NE = build(core, T, topo)
     if "o" not in _ORDER:
-        deps = depends(ops)
-        _ORDER["d"] = deps
-        _ORDER["o"], _ORDER["st"], _ORDER["fin"] = schedule(ops, deps)
-        _ORDER["ops"] = ops
+        _ORDER["c"], _ORDER["d"], _ORDER["o"] = plan(core, T, topo)[:3]
+    ops, NE = build(core, T, topo, _ORDER["c"])
     deps, order = _ORDER["d"], _ORDER["o"]
     eng = {"v": g.vector, "s": g.scalar, "t": g.tensor, "g": g, "y": g.sync}
     esem = {"v": "sv", "s": "ss", "t": "st", "g": "sg"}

from concourse.bass import DstId, RemoteDMATransfer
from concourse.mybir import AluOpType as A, ActivationFunctionType as F

NV, HOP = 3, 3
CFG = {"GA": 1.56, "SCA": 3.8, "PEC": 0.45, "WAKE": 130.0, "FIX": 0.0, "DM": 1.0,
       "CV": 128, "CS": 256, "CUT": (0, 1536), "XG": 8, "XV": 8, "PEN": 2000.0, "PENS": 1000.0,
       "SLACK": {"v": 0.0, "s": 0.0, "t": 0.0}, "SEED": 6, "NOISE": 300.0,
       "SPD": 0, "SPA": 1, "FBI": 6, "ORD": 1, "MM": 4, "VAR": (3,), "UG": 768, "SQ": 8}
CY = 0.83
MAGIC = 6442450944.0
SEG = 19
KW = 8 * SEG
SA, ZC, TB, SB, UW = 4096, 4224, 4232, 5256, 5384
C0, C1 = 1572864.0, 7864320.0
RR = 16384.0


def _scratch():
    s = {}

    def sb(n, c, d):
        s[n] = ("sbuf", [128, c], d)
    for n, c in (("pg", 4096), ("D", 4096), ("M", 4096), ("M1", 4096), ("xr", 4096), ("ef", 544), ("Wd", 16), ("Wm", 16),
                 ("W3", 144), ("pos", 64), ("npc", 256),
                 ("Wa", 24), ("Wt", KW), ("kc", 2 * KW), ("ke", 256), ("cst", 48), ("ones", KW), ("Id", 768), ("IW", 136),
                 ("Wb", 128), ("Q", 144), ("Sel", 1024), ("S2m", 384), ("W1", 144), ("W2", 144), ("dq", 576), ("eq", 1152),
                 ("es", 1152), ("x0s", 256), ("x1s", 256), ("x2s", 256), ("x3s", 256), ("z0", 256), ("z1", 256), ("z2", 256),
                 ("xo0", 256), ("xo1", 256), ("xo2", 256), ("tc", 768), ("ab", 6 * KW), ("bar", 6 * KW), ("tt", 256),
                 ("mx", 256), ("xf", 256), ("G2", 256), ("pay", 128), ("sg", 32), ("kb", 48)):
        sb(n, c, "bfloat16")
    for n, c in (("U", UW), ("idt", 5256), ("ic", 256), ("R", KW), ("Bm", KW), ("B128", 128), ("tmp", 2 * KW), ("D128", 128),
                 ("col", 40), ("cm", 1280), ("qc", 512), ("E", 256), ("Er", 512), ("rm", 2 * KW), ("sc", 8 * KW),
                 ("cv", 256), ("cvk", 384), ("VB", 416), ("FL", 320), ("NF", 320), ("c2", 192), ("P", 320), ("RS", 320),
                 ("SD0", 96), ("SD1", 96), ("SO", 96), ("thr", 16), ("gs", 8), ("gj", 16), ("A7", 1), ("Z", 24), ("spr", 16),
                 ("y1", 32), ("y2", 16), ("kcol", 256), ("G", 256), ("c13", 256), ("Cb", 512), ("mk", 256), ("dl", 256), ("t8", 80),
                 ("co0", 128), ("co1", 128), ("Wv0", 512), ("Wv1", 512), ("Wv2", 512)):
        sb(n, c, "float32")
    for n, c in (("ti", 1024), ("ai", 256), ("pi", 512), ("wi", 1), ("si", 16), ("ci", 8), ("vi", 256), ("ni", 256),
                 ("ki", 96), ("Ai", 2), ("ui", 256), ("u2", 256)):
        sb(n, c, "int32")
    for n, c in (("nu", 256), ("cl", 16), ("cs", 64), ("O", 16), ("lst", 192)):
        sb(n, c, "uint16")
    for n in ("K0", "K1", "A0", "A1", "C0", "C1", "B0", "B1"):
        s[n] = ("psum", [128, 512], "float32")
    return s


SCRATCH = _scratch()
NDMA = 30
SEMAPHORES = ["sv", "ss", "st", "sg", "ls", "rz"] + ["r%d%d" % (v, h) for v in range(NV) for h in range(2)] + \
    ["d%d" % i for i in range(NDMA)]
PSUM = ("K0", "K1", "A0", "A1", "C0", "C1", "B0", "B1")
_ORDER = {}


def build(core, T, topo, cuts):
    rank = T.rank_of(core)
    n = len(T.cores)
    ops = []
    nd = [0]
    last = {}
    GA, SCA, PEC, FIX, DM = CFG["GA"], CFG["SCA"], CFG["PEC"], CFG["FIX"], CFG["DM"]

    def S(name, lo=None, hi=None, step=None, p=None):
        t = T[name]
        if lo is None:
            lo, hi = 0, t.shape[1]
        ps = slice(None) if p is None else p
        if step is not None:
            hi = lo + (hi - 1 - lo) // step * step + 1
        ap = t[ps, lo:hi] if step is None else t[ps, lo:hi:step]
        cnt = (hi - lo + (step or 1) - 1) // (step or 1)
        return (ap, ((name, lo, hi),), cnt, t.dtype)

    def IND(win, off):
        return (win[0].indirect(off[0]), win[1] + off[1], off[2] * 16, "ind")

    def add(eng, fn, rd, wr, cost, key=None, kind="c", sem=None, lat=0.0, after=None, pen=0.0):
        r, w = [], []
        for x in rd:
            r += list(x[1])
        for x in wr:
            w += list(x[1])
        ops.append({"e": eng, "fn": fn, "r": r, "w": w, "c": cost + (FIX if eng in "vs" else 0.0), "key": key, "k": kind,
                    "sem": sem, "lat": lat, "after": after, "pen": pen, "ord": last.get(eng) if pen else None})
        if pen:
            last[eng] = len(ops) - 1
        return len(ops) - 1

    def two(x):
        return "16" in str(x[3])

    def aps(xs):
        return [x for x in xs if isinstance(x, tuple)]

    def a0(x):
        return x[0] if isinstance(x, tuple) else x

    def vcost(out, in0, base):
        if in0[3] == "ind":
            return 50 + in0[2] * GA * CY
        if out[3] == "ind":
            return 50 + out[2] * SCA * CY
        return max(64, base) * CY

    def tt(out, a, b, op, pen=0.0, key=None):
        ps = a[1][0][0] in PSUM or b[1][0][0] in PSUM
        add("v", lambda e: e.tensor_tensor(out[0], a[0], b[0], op), [a, b] + ([out] if out[3] == "ind" else []), [out],
            vcost(out, a, a[2] * (1 if ps else 2)), pen=pen, key=key)

    def ts(out, a, s1, op0, s2=None, op1=None, key=None):
        c = vcost(out, a, a[2] * (0.5 if two(a) and two(out) else 1))
        if op1 is None:
            add("v", lambda e: e.tensor_scalar(out[0], a[0], a0(s1), None, op0), aps([a, s1]), [out], c, key=key)
        else:
            add("v", lambda e: e.tensor_scalar(out[0], a[0], a0(s1), a0(s2), op0, op1), aps([a, s1, s2]), [out], c, key=key)

    def cp(out, a, key=None):
        add("v", lambda e: e.tensor_copy(out[0], a[0]), [a], [out], vcost(out, a, a[2] * (0.5 if two(a) and two(out) else 1)), key=key)

    def ms(out, c, key=None):
        add("v", lambda e: e.memset(out[0], c), [], [out], max(64, out[2] * (0.5 if two(out) else 1)) * CY, key=key)

    def scan(out, d0, d1, op0, op1):
        c = max(64, out[2] * (0.5 if two(out) and two(d0) and two(d1) else 1)) * CY
        add("v", lambda e: e.tensor_tensor_scan(out[0], d0[0], d1[0], 0.0, op0, op1), [d0, d1], [out], c)

    def act(out, a, f=F.Identity, bias=0.0, scale=1.0, key=None, pen=0.0, acc=None):
        c = 65 + a[2] * GA * CY if a[3] == "ind" else max(64, a[2]) * CY + 20
        if acc is None:
            add("s", lambda e: e.activation(out[0], a[0], f, bias=a0(bias), scale=a0(scale)), aps([a, bias, scale]), [out], c, key=key, pen=pen)
        else:
            add("s", lambda e: e.activation(out[0], a[0], f, bias=a0(bias), scale=a0(scale), accum_out=acc[0]), aps([a, bias, scale]), [out, acc], c + 20)

    def aff(eng, out, a, scale=1.0, bias=0.0, key=None):
        if eng == "s":
            act(out, a, bias=bias, scale=scale, key=key)
        else:
            ts(out, a, scale, A.mult, bias, A.add, key=key)

    def iota(out, pat, base, cm, key=None):
        if "int" in str(out[3]):
            add("g", lambda e: e.iota(out[0], pat, base, cm), [], [out], 130 + 2 * CY * out[2], key=key)
        else:
            add("g", lambda e: e.iota(out[0], pat, base, cm, allow_small_or_imprecise_dtypes=True), [], [out], 130 + 2 * CY * out[2], key=key)

    def sel(out, a, pat, op, fill, base, cm, key=None):
        add("g", lambda e: e.affine_select(out[0], a[0], pat, op, fill, base, cm), [a], [out], 170 + 2 * CY * out[2], key=key)

    def mm(lst, start=True, stop=True):
        m = CFG["MM"]
        if len(lst) > m:
            for q in range(0, len(lst), m):
                mm(lst[q:q + m], start and q == 0, stop and q + m >= len(lst))
            return

        def fn(e):
            for i, (o, l, r) in enumerate(lst):
                ins = e.matmul(o[0], l[0], r[0], start and i == 0, stop and i == len(lst) - 1)
            return ins
        add("t", fn, [x[1] for x in lst] + [x[2] for x in lst], [x[0] for x in lst],
            sum(max(min(64, x[1][2]), x[2][2]) * (1 if two(x[1]) else 4) for x in lst) * PEC, lat=60.0)

    def dma(out, in_, q="y", key=None, lat=2000.0):
        sem = "d%d" % nd[0]
        nd[0] += 1
        o = out if isinstance(out, tuple) else (out, (), 0, 0)
        i = in_ if isinstance(in_, tuple) else (in_, (), 0, 0)
        add(q, lambda e: e.dma_start(o[0], i[0]), [i], [o], 60.0, key=key, kind="d", sem=(sem, 16), lat=lat * DM)

    def send(pairs, sem, cnt):
        def fn(e):
            trs = []
            for j, (src, dst, r) in enumerate(pairs):
                c = T.cores[r % n]
                en = topo.engines(core, c)
                per = len(en) // len(pairs)
                m = 0
                for x in en[j * per:(j + 1) * per]:
                    m |= 1 << x
                rid, pid, _ = topo.addr(c)
                trs.append(RemoteDMATransfer(dst_ids=[DstId(rid=rid, pnc=pid)], dma_engine_mask=m, remote_sem=T.sem[sem], src=src[0], dst=dst[0]))
            return e.remote_dma_fused(trs, local_sem=T.sem.ls)
        i = add("g", fn, [x[0] for x in pairs], [], 600.0, kind="s")
        add("r", None, [], [x[1] for x in pairs], 0.0, kind="r", sem=(sem, cnt), lat=1500.0 * DM, after=i)

    NE = len(topo.engines(core, T.cores[(rank + HOP) % n]))
    p1 = slice(0, 1)
    row = lambda r: slice(r, 128, 16)

    dma(S("x0s"), T.x0[:])
    dma(S("wi"), T.wt[:], q="s")
    dma(S("ai"), T.act[:], q="s")
    dma(S("si"), T.start[:], q="s")
    for c in range(4):
        dma(S("pg", 1024 * c, 1024 * c + 1024), T.prog[:, 1024 * c:1024 * c + 1024], lat=2600.0 + 800 * c)
    dma(S("ti"), T.team[:], lat=5800.0)
    dma(S("z0"), T.goal[:], lat=5800.0)
    ms(S("ef"), 0.0)
    dma(S("ef", 16, 528), T.eff[:], lat=5800.0)

    ug = CFG["UG"]
    ms(S("U", 0, 4096 - ug), 1.0)
    iota(S("U", 4096 - ug, 4096), [[0, ug]], 1, 0)
    iota(S("U", SA, TB), [[0, TB - SA]], 0, 0)
    iota(S("U", SB, UW), [[0, UW - SB]], 0, 0)
    iota(S("ci", 0, 1), [[0, 1]], 0, 1)
    iota(S("ic"), [[1, 256]], 0, 0)
    ts(S("ci", 1, 2), S("ci", 0, 1), 15, A.bitwise_and)
    ts(S("ci", 2, 3), S("ci", 0, 1), 4, A.arith_shift_right)
    ts(S("ci", 3, 4), S("ci", 0, 1), 3, A.arith_shift_right, 1, A.bitwise_and)
    ts(S("ci", 4, 5), S("ci", 0, 1), 7, A.bitwise_and)
    cp(S("col", 0, 5), S("ci", 0, 5))
    col = lambda i: S("col", i, i + 1)
    lc, bc, hc, l8 = col(1), col(2), col(3), col(4)
    ts(S("pi", 0, 256), S("ai"), 63, A.bitwise_and)
    ts(S("pi", 256, 512), S("ai"), 6, A.arith_shift_right)
    cp(S("cm", 0, 512), S("pi"))
    iota(S("cm", 512, 768), [[0, 4], [1, 64]], 0, 0)
    iota(S("dl"), [[1, 4], [0, 64]], 0, 0)
    aff("s", col(7), lc, 4.0)
    act(S("cm", 768, 1024), S("dl"), bias=col(7))
    cp(S("cm", 1024, 1280), S("ai"))
    for r in (2, 3, 0, 1, 4):
        dma(S("U", 0, 4096, p=row(2 + r)), S("cm", 256 * r, 256 * r + 256), key="U")
    aff("v", col(5), hc, 64.0, 8.0)
    aff("v", col(6), bc, 8.0, col(5))
    ts(S("Q"), S("ic", 0, 144), col(6), A.is_equal)
    for c in range(8):
        act(S("M", 512 * c, 512 * c + 512), S("pg", 512 * c, 512 * c + 512), F.Square, bias=-7.5)
        mm([(S("A1"), S("Q", 8 - c, 136 - c), S("M", 512 * c, 512 * c + 512))], start=c == 0, stop=c == 7)
    act(S("qc"), S("A1"))
    dma(S("U", 0, 4096, p=row(0)), S("qc", 0, 512, p=slice(0, 64)), key="U")
    dma(S("U", 0, 4096, p=row(1)), S("qc", 0, 512, p=slice(64, 128)), key="U", q="s")

    def fill(out, c, key=None, p=None):
        sel(out, S("ic", 0, out[2], p=p), [[0, out[2]]], A.is_gt, c, 0, 0, key=key)
    iota(S("ones"), [[0, KW]], 1, 0)
    for nm, w in (("B128", 16), ("Bm", SEG)):
        sel(S(nm), S("ones", 0, 8 * w), [[-16, 8], [0, w]], A.is_ge, 0.0, 0, 1)
        sel(S(nm), S(nm), [[16, 8], [0, w]], A.is_ge, 0.0, 15, -1)
    B8 = S("B128", 0, 128, 16)
    ts(col(8), S("wi"), 2.0, A.mult)
    aff("v", S("Wb"), S("B128"), col(8))
    cp(S("cl"), S("si"))
    cp(S("U", TB, SB), S("ti"))
    aff("v", S("Wd", 0, 8), B8, -2048.0)
    aff("v", S("Wd", 8, 16), B8, -131072.0)
    ts(col(9), lc, 1.5, A.is_lt, 2048.0, A.mult)
    for j, (w, r) in enumerate((("Wm", 2), ("Wm", 3))):
        ts(col(10 + j), lc, float(r), A.is_equal, col(9), A.add)
        ts(S(w, 8 * (j % 2), 8 * (j % 2) + 8), B8, col(10 + j), A.mult, 64.0 if j % 2 else 1.0, A.mult)
    ts(col(14), lc, 3.0, A.is_equal, 64.0, A.mult)
    ts(col(15), lc, 2.0, A.is_equal, col(14), A.add)
    for j in range(3):
        aff("v", S("Wa", 8 * j, 8 * j + 8), B8, col(15))
    ts(col(16), lc, 5.0, A.is_equal, -64.0, A.mult)
    ts(col(17), lc, 4.0, A.is_equal)
    tt(col(18), col(16), col(17), A.subtract)
    ts(col(19), lc, 7.0, A.is_equal)
    aff("v", S("Wt"), S("Bm"), col(18))
    for j in (16, 17, 18):
        aff("v", S("Wt", j, KW, SEG), B8, col(19))
    sel(S("IW"), S("ones", 0, 136), [[-1, 136]], A.is_equal, 0.0, 2, 1)
    Ip = S("IW", 2, 130)
    Id = lambda j: S("Id", 128 * j, 128 * j + 128)
    for j, c in enumerate((2.0 ** 24, 2.0 ** 30, -C1, -64 * C1, -1024.0)):
        aff("v", Id(j), Ip, c)
    iota(S("kc", 0, KW, p=p1), [[0, 8], [128, SEG]], 0, 0)
    iota(S("kc", KW, 2 * KW, p=p1), [[0, 8], [8192, SEG]], 0, 0)
    iota(S("rm"), [[0, 2 * KW]], 0, 0)
    fill(S("rm", 0, 2 * KW, SEG), 2.0 ** 40, key="rm")
    fill(S("kc", 17, 2 * KW, SEG, p=p1), 2.0 ** 38, key="kc", p=p1)
    fill(S("kc", 18, 2 * KW, SEG, p=p1), 2.0 ** 38, key="kc", p=p1)
    for f in range(2):
        m = 64.0 ** f
        fill(S("kc", KW * f + 16, KW * f + KW, SEG, p=p1), C0 * m, key="kc", p=p1)
        fill(S("rm", KW * f + 17, KW * f + KW, SEG), 1.5 * 2.0 ** 30 * m, key="rm")
        fill(S("rm", KW * f + 18, KW * f + KW, SEG), -1.5 * 2.0 ** 30 * m, key="rm")
    for j, c in enumerate((C1, 64 * C1, 1024.0, 2048.0)):
        fill(S("cst", 8 * j, 8 * j + 8, p=p1), c, key="cst", p=p1)
    iota(S("ke", 0, 256, p=p1), [[288, 2], [0, 128]], -255, 0)
    iota(S("D128"), [[0, 8], [1, 16]], 0, 0)
    ts(S("D128"), S("D128"), lc, A.is_equal)
    for b in range(8):
        aff("s", S("Sel", 128 * b, 128 * b + 128), S("D128"), S("B128", 16 * b, 16 * b + 1))
    aff("v", S("O", 0, 1), l8, 8.0, bc)
    ts(col(20), l8, 3.0, A.add, l8, A.mult)
    aff("v", S("O", 2, 3), col(20), 8.0, 15.0)
    lt = lambda lo, hi, st=None: S("tmp", lo, hi, st)
    iota(lt(0, 40), [[1, 8], [0, 5]], 208, 0)
    iota(lt(2, 40, 5), [[1, 8]], 224, 0)
    iota(lt(40, 120), [[0, 2], [8, 8], [64, 5]], 1024 - 128, 0)
    iota(lt(40, 120, 5), [[0, 2], [1, 8]], 216, 0)
    iota(lt(41, 120, 5), [[0, 2], [1, 8]], 192, 0)
    iota(lt(120, 176), [[0, 56]], 0, 0)
    iota(lt(128, 168), [[24, 8], [8, 5]], 1024 - 8, 0)
    iota(lt(128, 168, 5), [[0, 8]], 0, 0)
    iota(lt(132, 168, 5), [[0, 8]], 0, 0)
    iota(S("P", 0, 176), [[0, 11], [1, 16]], 0, 0)
    sel(S("NF", 0, 176), S("P", 0, 176), [[0, 11], [1, 16]], A.is_equal, 1.0, 0, 0)
    ts(S("P", 0, 176), S("P", 0, 176), lc, A.is_equal)
    tt(S("FL", 0, 176), S("P", 0, 176), lt(0, 176), A.mult)
    scan(S("RS", 0, 176), S("NF", 0, 176), S("FL", 0, 176), A.mult, A.add)
    aff("s", col(26), bc, 1.0, -1024.0)
    ts(S("RS", 176, 187), S("RS", 15, 176, 16), 512.0, A.is_gt, col(26), A.mult)
    tt(S("RS", 192, 203), S("RS", 176, 187), S("RS", 15, 176, 16), A.add)
    cp(S("O", 4, 15), S("RS", 192, 203))
    OA, OE, OW, OK = S("O", 0, 1), S("O", 2, 3), S("O", 4, 12), S("O", 12, 15)
    aff("v", col(21), bc, 16.0, 15.0)
    ts(S("W1"), S("ic", 0, 144), col(21), A.is_equal)
    aff("v", S("W2"), S("W1"), -2.0)
    aff("v", S("W3"), S("W1"), col(18))
    iota(S("cvk", 0, 64), [[256, 8], [0, 8]], 0, 0)
    aff("s", col(25), lc, 16.0)
    act(S("pos"), S("cvk", 0, 64), bias=col(25))
    ts(col(22), col(18), 0.0, A.not_equal)
    aff("s", S("S2m", 0, 128), S("IW", 4, 132), col(22))
    aff("s", S("S2m", 128, 256), S("IW", 0, 128), col(17))
    aff("s", col(23), col(16), -1.0)
    aff("s", S("S2m", 256, 384), S("IW", 1, 129), col(23))
    aff("s", S("Z", 0, 16), S("D128", 0, 16))
    ts(col(24), col(15), 0.0, A.not_equal)
    ts(S("Z", 16, 24), S("ones", 0, 8), lc, A.mult, 6.0, A.is_equal)
    aff("v", S("Z", 16, 17), S("Z", 17, 18), 1.0, col(24))
    iota(S("dq"), [[0, 576]], 1, 0)
    for j in range(8):
        o = 8 * j * (j + 1)
        aff("s", S("dq", o + 16 * j, o + 16 * j + 16), S("D128", 0, 16), RR - 1.0, 1.0)
        iota(S("dq", o, o + 1), [[0, 1]], 0, 0)
    iota(S("y1", 0, 16), [[0, 2], [16, 8]], 0, 0)
    act(S("y1", 0, 16), S("y1", 0, 16), bias=lc)
    aff("s", S("spr"), S("y1", 0, 16), 1.0 / RR, SB / RR)
    for nm in ("c2", "SD0", "SD1", "co0", "co1"):
        iota(S(nm), [[0, T[nm].shape[1]]], 0, 0)
    for h in range(2):
        iota(S("Wv0", 256 * h + 192, 256 * h + 256), [[0, 64]], 0, 0)
        for nm, o in (("Wv0", 256 * h + 192), ("co0", 64 * h), ("co1", 64 * h)):
            aff("s", S(nm, o + 16, o + 24), S("y1", 0, 8), 1.0, float(SA))
            aff("s", S(nm, o + 24, o + 32), S("y1", 0, 8), 1.0, float(SA - TB))
        aff("s", S("SD1", 48 * h + 17, 48 * h + 32, 2), S("y1", 0, 8))
        aff("s", S("SD0", 48 * h + 17, 48 * h + 32, 2), S("y1", 0, 8), 0.0, 128.0)
    send([(S("z0"), S("z1"), rank + HOP), (S("z0"), S("z2"), rank + 2 * HOP)], "rz", NE)
    for c in range(8):
        iota(S("idt", 657 * c, 657 * c + 657), [[1, 657]], 657 * c, 0)

    def tolist(out, c0, width, rhs):
        mm([(S(out, c0 + width * b, c0 + width * b + width), S("Sel", 128 * b, 128 * b + 128), r) for b in range(8) for r in rhs])

    def gain(h, xo, mx):
        mm([(S("K%d" % h, 0, 8), S(w, 15 - l, 143 - l), S(x[1][0][0], x[1][0][1] + l, x[1][0][2], 16))
            for w, x in (("W1", xo), ("W2", mx)) for l in range(16)])

    def prep(v, h):
        a, b = 128 * h, 128 * h + 128
        x, z = S("x%ds" % v, a, b), S("z%d" % v, a, b)
        Kk, Bk = "K%d" % h, "B%d" % h
        one = S("ones", 0, 128, p=p1)
        act(S(Bk, 384, 512), z)
        if v == 0:
            cp(S("Wv0", 256 * h + 192, 256 * h + 200), S("si", 8 * h, 8 * h + 8))
        else:
            cp(S("cl", 8 * h, 8 * h + 8), S("Wv%d" % v, 256 * h + 192, 256 * h + 200))
        mm([(S(Kk, 0, 128), S("Wb"), x), (S(Kk, 128, 256), S("Wb"), x),
            (S(Kk, 0, 128), one, S("ke", 0, 128, p=p1)), (S(Kk, 128, 256), one, S("ke", 128, 256, p=p1))])
        act(S("Er", a, b), S(Kk, 0, 128), bias=MAGIC)
        act(S("Er", 256 + a, 256 + b), S("Er", a, b), bias=-MAGIC)
        tt(S("E", a, b), S(Kk, 128, 256), S("Er", 256 + a, 256 + b), A.subtract)
        xg, xv = (CFG["XG"], CFG["XV"]) if v else (0, 16 if h else 0)
        for k in range(16 - xg):
            aff("v" if k < xv else "s", S("xr", 16 * a + k, 16 * b, 16), x, 2.0, -15.0, key="xr%d" % v)
        if xg:
            act(S("xf", a, b), x, bias=-15.0, scale=2.0)
        for k in range(16 - xg, 16):
            sel(S("xr", 16 * a + k, 16 * b, 16), S("xf", a, b), [[0, 128]], A.is_ge, 0.0, 0, 0, key="xr%d" % v)
        act(S("Cb", 256 * h, 256 * h + 128), S("E", a, b), bias=-1599.5, scale=48.5)

    def bar_of_success(v, h):
        a, b = 128 * h, 128 * h + 128
        thr = S("thr", 8 * h, 8 * h + 8)
        if v == 0:
            tt(S("mx", a, b), S("x0s", a, b), S("B%d" % h, 384, 512), A.max)
            gain(h, S("x0s", a, b), S("mx", a, b))
            act(thr, S("K%d" % h, 0, 8))
            return
        if h == 1:
            mm([(S("C1", 256, 257), S("B128"), S("gs", j, j + 1)) for j in range(2 * v)])
            cp(S("Ai", 0, 1), S("C1", 256, 257))
            ts(S("Ai", 1, 2), S("Ai", 0, 1), 7, A.bitwise_and)
            cp(S("A7"), S("Ai", 1, 2))
        act(thr, S("Wv%d" % v, 256 * h + 200, 256 * h + 208), bias=S("A7"))

    def step(v, h, s):
        a, b = 128 * h, 128 * h + 128
        Kk, Ak, Bk, Ck = "K%d" % h, "A%d" % h, "B%d" % h, "C%d" % h
        one = S("ones", 0, 128, p=p1)
        cur = S("cl", 8 * h, 8 * h + 8) if s == 1 else S("cs", 32 * h + 16 * (s - 2), 32 * h + 16 * (s - 2) + 8)
        tt(S("vi", a, b), IND(S("U", TB, SB) if v else S("ti"), cur), S("E", a, b), A.mult)
        ts(S("ni", a, b), S("vi", a, b), 5, A.arith_shift_right, 4095, A.bitwise_and)
        cp(S("nu", a, b), S("ni", a, b))
        t0 = 384 * h
        Mb = "M1" if s == 1 else "M"
        act(S("tc", t0 + 128 * (s - 1), t0 + 128 * s), IND(S("U", 0, 1024), cur))
        o = 2048 * h
        for c in cuts.get(("s", v, h, s), (CFG["CS"],) * (2048 // CFG["CS"])):
            act(S(Mb, o, o + c), IND(S("U", 0, 4096), S("nu", o // 16, (o + c) // 16)), pen=CFG["PENS"])
            ops[-1]["run"] = ("s", v, h, s, o, c)
            o += c
        o = 2048 * h
        for c in cuts.get(("v", v, h, s), (CFG["CV"],) * (2048 // CFG["CV"])):
            tt(S("D", o, o + c), IND(S("pg"), S("nu", o // 16, (o + c) // 16)), S("xr", o, o + c), A.mult, pen=CFG["PEN"])
            ops[-1]["run"] = ("v", v, h, s, o, c)
            o += c
        o = 2048 * h

        def sums(bank, w, src, wt, split):
            if not split:
                return [(S(bank, k, w, SEG), S(src, o + k, o + 2048, 16), wt) for k in range(16)], []
            return ([(S(bank, k, w, SEG, p=slice(0, 96)), S(src, o + k, o + 1536, 16), wt) for k in range(16)],
                    [(S(bank, k, w, SEG, p=slice(96, 128)), S(src, o + 1536 + k, o + 2048, 16), wt) for k in range(16)])
        mm([(S(Ak, KW * j, KW * j + KW), S("tc", t0 + 128 * j, t0 + 128 * j + 128), S("Wt")) for j in range(s)], stop=False)
        la, lb = sums(Ak, KW * s, Mb, S("Wa", 0, 8 * s), CFG["SPA"])
        mm(la, start=False)
        if lb:
            mm(lb, start=False)
        b0 = 3 * KW * h
        if s in CFG["VAR"]:
            ts(S("bar", b0, b0 + KW * s), S(Ak, 0, KW * s), 0.0, A.is_equal)
        else:
            act(S("ab", b0, b0 + KW * s), S(Ak, 0, KW * s), F.Abs)
            act(S("bar", b0, b0 + KW * s), S("ab", b0, b0 + KW * s), F.Relu, bias=1.0, scale=-1.0)
        pay = lambda i: S("pay", 64 * h + 16 * i, 64 * h + 16 * i + 16)

        def keys(bank, wm, carry):
            mm([(S(bank, 0, 2 * KW), one, S("kc", 0, 2 * KW, p=p1))] + carry, stop=False)
            mm(sums(bank, 2 * KW, Mb, S(wm), 0)[0], start=False, stop=False)
            lst = [(S(bank, KW * f, KW * f + KW), Id(f), S("bar", b0 + KW * j, b0 + KW * j + KW)) for j in range(s) for f in range(2)]
            la, lb = sums(bank, 2 * KW, "D", S("Wd"), CFG["SPD"] and bank == Kk)
            mm(la, start=False, stop=False)
            mm(lst, start=False)
            if lb:
                mm(lb, start=False)
        both, hi = S(Kk, 16, 2 * KW, SEG), S(Kk, KW + 16, 2 * KW, SEG)
        if s == 1:
            carry = [(both, one, S("cst", 0, 16, p=p1)), (hi, one, S("cst", 24, 32, p=p1))]
        else:
            sg = S("sg", 16 * h + 8 * (s - 2), 16 * h + 8 * (s - 2) + 8)
            carry = [(hi, one, S("cst", 16, 24, p=p1)), (both, Ip, pay(s - 1)), (S(Kk, 16, KW, SEG), Id(2), sg), (hi, Id(3), sg), (hi, Id(4), sg)]
        keys(Kk, "Wm", carry)
        c0 = 4 * KW * h + KW * (s - 1)
        scan(S("sc", c0, c0 + 2 * KW), S("rm"), S(Kk, 0, 2 * KW), A.add, A.min)
        tt(pay(s), S("sc", c0 + 16, c0 + 2 * KW, SEG), S("sc", c0 + 18, c0 + 2 * KW, SEG), A.subtract)
        p0 = 64 * h + 16 * s
        tolist(Ck, 0, 8, [S("pay", p0, p0 + 8), S("pay", p0 + 8, p0 + 16)])
        cva = S("Wv%d" % v, 256 * h + 64 * (s - 1), 256 * h + 64 * s)
        act(cva, S(Ck, 0, 64))
        if s < 3:
            ts(S("cs", 32 * h + 16 * (s - 1), 32 * h + 16 * s), IND(cva, OA), 1023.0, A.min)
            act(S("sg", 16 * h + 8 * (s - 1), 16 * h + 8 * s), S("pay", p0 + 8, p0 + 16), F.Sign, bias=-1000.0)
        else:
            ts(S("lst", 96 * h, 96 * h + 16), IND(cva, OA), -1008.0, A.add, 528.0, A.min)
        if s == 1:
            q = 48 * h
            cp(S("ki", q, q + 8), S("sc", c0 + 18, c0 + KW, SEG))
            ts(S("ki", q + 24, q + 32), S("ki", q, q + 8), 7, A.arith_shift_right, 15, A.bitwise_and)
            cp(S("kb", 24 * h, 24 * h + 8), S("ki", q + 24, q + 32))
            mm([(S(Bk, 0, 64), Ip, S("pos"))], stop=False)
            mm([(S(Bk, 8 * j, 8 * j + 8), S("Sel", 128 * j, 128 * j + 128), S("kb", 24 * h, 24 * h + 8)) for j in range(8)], start=False)
            act(S("cv", a, a + 64), S(Bk, 0, 64))
            cp(S("lst", 96 * h + 80, 96 * h + 96), IND(S("cv", a, a + 64), OA))
            act(S("npc", a, b), IND(S("M1", o, o + 2048), S("lst", 96 * h + 80, 96 * h + 88)))
            mm([(S(Bk, 64, 72), S("W3", 15 - l, 143 - l), S("npc", a + l, b, 16)) for l in range(16)])
            act(S("Wv%d" % v, 256 * h + 224, 256 * h + 232), S(Bk, 64, 72), scale=-1.0)

    def post(v, h):
        a, b = 128 * h, 128 * h + 128
        Kk, Ak, Bk, Ck = "K%d" % h, "A%d" % h, "B%d" % h, "C%d" % h
        x = S("x%ds" % v, a, b)
        lst = lambda i, j=1: S("lst", 96 * h + 8 * i, 96 * h + 8 * (i + j))
        v0, f0, s0 = 208 * h, 160 * h, 48 * h
        xo = S("xo%d" % v, a, b)
        tt(S("tt", a, b), IND(S("ef"), lst(0)), x, A.subtract)
        act(xo, S("tt", a, b), F.Abs)
        tt(S("mx", a, b), xo, S(Bk, 384, 512), A.max)
        gain(h, xo, S("mx", a, b))
        thr = S("thr", 8 * h, 8 * h + 8)
        tt(S("SD1", s0, s0 + 16, 2), S(Kk, 0, 8), thr, A.is_gt, key="g%d%d" % (v, h))
        cp(S("ki", s0 + 8, s0 + 24), S("sc", 4 * KW * h + KW + 18, 4 * KW * h + 3 * KW, SEG))
        ts(S("ki", s0 + 32, s0 + 48), S("ki", s0 + 8, s0 + 24), 7, A.arith_shift_right, 15, A.bitwise_and)
        cp(S("kb", 24 * h + 8, 24 * h + 24), S("ki", s0 + 32, s0 + 48))
        tolist(Ak, 0, 24, [S("kb", 24 * h, 24 * h + 24)])
        act(S("cvk", 192 * h, 192 * h + 192), S(Ak, 0, 192))
        act(S("VB", v0 + 128, v0 + 176), IND(S("cvk", 192 * h, 192 * h + 192), OK))
        act(S("VB", v0, v0 + 128), IND(S("Wv%d" % v, 256 * h, 256 * h + 256), OW))
        ts(S("FL", f0, f0 + 80), S("VB", v0 + 40, v0 + 120), 1024.0, A.is_lt)
        ts(S("c2", 96 * h, 96 * h + 80), S("VB", v0 + 40, v0 + 120), 2048.0, A.is_lt)
        tt(S("FL", f0 + 80, f0 + 160), S("FL", f0, f0 + 80), S("c2", 96 * h + 1, 96 * h + 81), A.mult)
        act(S("NF", f0, f0 + 160), S("FL", f0, f0 + 160), bias=1.0, scale=-1.0)
        tt(S("P", f0, f0 + 120), S("FL", f0, f0 + 120), S("VB", v0, v0 + 120), A.mult)
        scan(S("RS", f0, f0 + 120), S("NF", f0, f0 + 120), S("P", f0, f0 + 120), A.mult, A.add)
        tt(S("P", f0 + 120, f0 + 160), S("FL", f0 + 120, f0 + 160), S("VB", v0 + 128, v0 + 168), A.mult)
        scan(S("RS", f0 + 120, f0 + 160), S("NF", f0 + 120, f0 + 160), S("P", f0 + 120, f0 + 160), A.mult, A.add)
        kg, L, kf, ks = S("RS", f0 + 2, f0 + 40, 5), S("RS", f0 + 44, f0 + 80, 5), S("RS", f0 + 83, f0 + 120, 5), S("RS", f0 + 123, f0 + 160, 5)
        kfo = S("SD1", s0 + 1, s0 + 16, 2)
        act(kfo, kf, bias=float(TB), key="g%d%d" % (v, h))
        tt(S("SD0", s0 + 1, s0 + 16, 2), kg, kfo, A.subtract)
        cp(lst(2), L)
        if v < NV - 1:
            co = "co%d" % v
            act(S(co, 64 * h, 64 * h + 8), L)
            act(S(co, 64 * h + 8, 64 * h + 16), S(Kk, 0, 8))
            send([(xo, S("x%ds" % (v + 1), a, b), rank + HOP), (S(co, 64 * h, 64 * h + 64), S("Wv%d" % (v + 1), 256 * h + 192, 256 * h + 256), rank + HOP)],
                 "r%d%d" % (v, h), NE)
        else:
            send([(xo, S("x3s", a, b), rank - HOP * v)], "r%d%d" % (v, h), NE)
            dma(T.yx[:, a:b], S("x3s", a, b))
        scan(S("SO", s0, s0 + 16), S("SD0", s0, s0 + 16), S("SD1", s0, s0 + 16), A.mult, A.add)
        key = S("SO", s0 + 1, s0 + 16, 2)
        cp(lst(3), key)
        act(S("kcol", a, b), IND(S("idt"), lst(3)))
        e0 = 576 * h
        for j in range(8):
            o = e0 + 8 * j * (j + 1)
            ts(S("eq", o, o + 16 * j + 16), S("kcol", a, a + 16 * j + 16), S("SO", s0 + 2 * j + 1, s0 + 2 * j + 2), A.is_equal)
        scan(S("es", e0, e0 + 576), S("dq"), S("eq", e0, e0 + 576), A.mult, A.max)
        tt(S("y1", 16 * h, 16 * h + 16), IND(S("es", e0, e0 + 576), OE), S("spr"), A.mult)
        tt(S("y2", 8 * h, 8 * h + 8), S("y1", 16 * h, 16 * h + 8), key, A.max)
        cp(lst(4), S("y2", 8 * h, 8 * h + 8))
        ts(lst(5), key, float(ZC), A.max)
        gd = S("SD1", s0, s0 + 16, 2)
        if v < NV - 1:
            act(S("SD1", s0 + 16, s0 + 32, 2), gd, acc=S("gs", 2 * v + h, 2 * v + h + 1))
        else:
            act(S("SD1", s0 + 16, s0 + 32, 2), gd)
        act(S("SD1", s0 + 32, s0 + 48, 2), gd)
        act(S("SD1", s0 + 33, s0 + 48, 2), ks)
        act(S("SD0", s0 + 33, s0 + 48, 2), ks, bias=16.0, scale=-1.0)
        scan(S("SO", s0 + 16, s0 + 48), S("SD0", s0 + 16, s0 + 48), S("SD1", s0 + 16, s0 + 48), A.mult, A.add)
        cp(lst(6, 2), S("SO", s0 + 17, s0 + 48, 2))
        act(S("G2", a, b), IND(S("U", 0, 1024), lst(2)))
        mm([(S(Ck, 128, 256), S("S2m", 128 * j, 128 * j + 128), S("G2", a, b)) for j in range(3)])
        act(S("Cb", 256 * h + 128, 256 * h + 256), S(Ck, 128, 256))
        act(S("c13", a, b), IND(S("U", 0, SB), lst(5)), scale=13.0)
        act(S("G", a, b), IND(S("U", 0, SB), lst(3)))
        act(S(Bk, 0, 128), S("G", a, b))
        act(S("mk", a, b), IND(S("Z"), lst(7)))
        tt(S("ui", a, b), IND(S("Cb", 256 * h, 256 * h + 256), lst(6)), S("c13", a, b), A.add)
        ts(S("u2", a, b), S("ui", a, b), 4095, A.bitwise_and)
        tt(S(Ak, 256, 384), S("u2", a, b), S(Bk, 0, 128), A.subtract)
        tt(S("dl", a, b), S("mk", a, b), S(Ak, 256, 384), A.mult)

    for v in range(NV):
        for h in (1, 0):
            prep(v, h)
        for h in (1, 0):
            if v == 0:
                bar_of_success(v, h)
        for s in range(1, 4):
            for h in (1, 0):
                step(v, h, s)
                if v and s == 1:
                    bar_of_success(v, h)
        for h in (1, 0):
            post(v, h)
        for h in (1, 0):
            tt(IND(S("U"), S("lst", 96 * h + 32, 96 * h + 40)), S("dl", 128 * h, 128 * h + 128), S("G", 128 * h, 128 * h + 128), A.add)
    dma(T.yteam[:, 0:512], S("U", TB, TB + 512), lat=2800.0)
    dma(T.yteam[:, 512:1024], S("U", TB + 512, SB), q="s", lat=2800.0)
    dma(T.yact[:], S("U", 0, 4096, p=row(6)), lat=2300.0)
    return ops, NE


def depends(ops):
    hist = {}
    deps = []
    for i, o in enumerate(ops):
        d = set()
        if o["after"] is not None:
            d.add(o["after"])
        acc = [(x, False) for x in o["r"]] + [(x, True) for x in o["w"]]
        for (nm, lo, hi), wr in acc:
            ps = nm in PSUM
            for (l2, h2, w2, j) in hist.get(nm, ()):
                if ps:
                    if wr or w2 or ops[j]["e"] != o["e"]:
                        d.add(j)
                elif (wr or w2) and l2 < hi and lo < h2 and not (o["key"] and o["key"] == ops[j]["key"]):
                    d.add(j)
        for (nm, lo, hi), wr in sorted(set(acc)):
            hs = hist.setdefault(nm, [])
            if wr and nm in PSUM:
                hs[:] = [y for y in hs if y[3] == i]
            hs.append((lo, hi, wr, i))
        d.discard(i)
        deps.append(d)
    anc = []
    for i, d in enumerate(deps):
        m = 0
        for j in d:
            m |= anc[j]
        deps[i] = sorted(j for j in d if not m >> j & 1)
        for j in d:
            m |= 1 << j
        anc.append(0 if ops[i]["k"] in "sr" else m)
    return deps


def schedule(ops, deps, order=None, first=None, fbi=0):
    n = len(ops)
    wake = CFG["WAKE"]
    pe = [o["e"] == "t" for o in ops]
    soft = [o["ord"] if CFG["ORD"] and order is None and o["ord"] is not None and o["ord"] not in deps[i] else None for i, o in enumerate(ops)]
    deps = [d if soft[i] is None else d + [soft[i]] for i, d in enumerate(deps)]
    succ = [[] for _ in range(n)]
    for i in range(n):
        for j in deps[i]:
            succ[j].append(i)

    def gap(j, i):
        return 0.0 if soft[i] == j or (pe[i] and pe[j]) else wake + ops[j]["lat"]
    fin = [0.0] * n
    st = [0.0] * n
    free = {}
    if order is not None:
        for i in order:
            e = ops[i]["e"]
            st[i] = max([free.get(e, 0.0)] + [fin[j] + (-60.0 if pe[i] and pe[j] else wake) for j in deps[i]])
            free[e] = st[i] + ops[i]["c"]
            fin[i] = free[e] + ops[i]["lat"]
        return order, st, fin
    pr = [0.0] * n
    for i in range(n - 1, -1, -1):
        pr[i] = ops[i]["c"] + max([pr[j] + gap(i, j) for j in succ[i]] + [ops[i]["lat"]])
    r = CFG["SEED"] * 7919 + 1
    for i in range(n):
        r = (r * 1103515245 + 12345) % 2147483648
        pr[i] += CFG["NOISE"] * r / 2147483648.0 - ops[i]["pen"]
    left = [len(d) for d in deps]
    rdy = [0.0] * n
    ready = {}
    for i in range(n):
        if not left[i]:
            ready.setdefault(ops[i]["e"], []).append(i)
    order = []
    prev = {}
    if first is not None:
        order, st, fin = schedule(ops, deps, first)
    while len(order) < n:
        best = None
        for e, l in ready.items():
            if not l:
                continue
            t = max(free.get(e, 0.0), min(rdy[i] for i in l))
            if best is None or t < best[0]:
                best = (t, e)
        t, e = best
        i = max((i for i in ready[e] if rdy[i] <= t + CFG["SLACK"].get(e, 40.0)), key=lambda i: (pr[i], -i))
        ready[e].remove(i)
        st[i] = max(t, rdy[i])
        ru = ops[i].get("run")
        if ru and prev.get(e) == ops[i]["ord"] and ru[4] % 2048 not in CFG["CUT"] and st[i] <= free[e] + 1.0:
            ops[i]["c"] -= 50.0 if e == "v" else 65.0
            ops[i]["join"] = True
        prev[e] = i
        free[e] = st[i] + ops[i]["c"]
        fin[i] = free[e] + ops[i]["lat"]
        order.append(i)
        for j in succ[i]:
            rdy[j] = max(rdy[j], free[e] + gap(i, j))
            left[j] -= 1
            if not left[j]:
                ready.setdefault(ops[j]["e"], []).append(j)

    def place(seq, pred, fwd):
        s0 = [0.0] * n
        lines = {}
        for i in seq:
            c = ops[i]["c"]
            t = 0.0 if fwd else ops[i]["lat"]
            for j in pred[i]:
                t = max(t, s0[j] + ops[j]["c"] + (gap(j, i) if fwd else gap(i, j)))
            ln = lines.setdefault(ops[i]["e"], [])
            lo, hi = 0, len(ln)
            while lo < hi:
                m = (lo + hi) // 2
                if ln[m][1] <= t:
                    lo = m + 1
                else:
                    hi = m
            while lo < len(ln) and ln[lo][0] < t + c - 1e-6:
                t = max(t, ln[lo][1])
                lo += 1
            ln.insert(lo, (t, t + c))
            s0[i] = t
        return s0
    best = (max(fin), order, st, fin)
    for _ in range(fbi):
        sb = place(sorted(range(n), key=lambda i: (-st[i] - ops[i]["c"], -i)), succ, False)
        st = place(sorted(range(n), key=lambda i: (-sb[i] - ops[i]["c"], i)), deps, True)
        fin = [st[i] + ops[i]["c"] + ops[i]["lat"] for i in range(n)]
        if max(fin) < best[0]:
            best = (max(fin), sorted(range(n), key=lambda i: (st[i], i)), st, fin)
    return best[1:]


def plan(core, T, topo):
    ops, _ = build(core, T, topo, {})
    order, st, fin = schedule(ops, depends(ops), fbi=0)
    cuts, head, kept = {}, {}, []
    for i, o in enumerate(ops):
        ru = o.get("run")
        if ru and o.get("join"):
            cuts[ru[:4]][-1] += ru[5]
            continue
        if ru:
            cuts.setdefault(ru[:4], []).append(ru[5])
        head[i] = len(kept)
        kept.append(i)
    ops, _ = build(core, T, topo, cuts)
    deps = depends(ops)
    order, st, fin = schedule(ops, deps, first=[head[i] for i in order if i in head], fbi=CFG["FBI"])
    return cuts, deps, order, st, fin


def rank_program(g, core, T, topo):
    if T.rank_of(core) is None:
        return
    if "o" not in _ORDER:
        _ORDER["c"], _ORDER["d"], _ORDER["o"] = plan(core, T, topo)[:3]
    ops, NE = build(core, T, topo, _ORDER["c"])
    deps, order = _ORDER["d"], _ORDER["o"]
    eng = {"v": g.vector, "s": g.scalar, "t": g.tensor, "g": g, "y": g.sync}
    esem = {"v": "sv", "s": "ss", "t": "st", "g": "sg"}
    n = len(ops)
    pos = [0] * n
    for p, i in enumerate(order):
        pos[i] = p
    need = [None] * n
    seen = {e: {} for e in eng}
    know = [None] * n
    used = set()
    for i in order:
        o = ops[i]
        if o["k"] == "r":
            know[i] = {}
            continue
        k = seen[o["e"]]
        w = {}
        for j in deps[i]:
            p = ops[j]
            if p["k"] == "s" or (p["e"] == "t" and o["e"] == "t"):
                continue
            s = p["sem"][0] if p["sem"] else esem[p["e"]]
            if k.get(s, -1) < pos[j] and (s not in w or pos[w[s]] < pos[j]):
                w[s] = j
        ws = sorted(w.items(), key=lambda x: -pos[x[1]])
        need[i] = []
        for s, j in ws:
            if k.get(s, -1) < pos[j]:
                need[i].append((s, j))
                used.add(j)
                k[s] = pos[j]
                for s2, p2 in know[j].items():
                    if k.get(s2, -1) < p2:
                        k[s2] = p2
        know[i] = dict(k)
    cnt = {}
    val = [0] * n
    for i in order:
        o = ops[i]
        if o["k"] == "c" and i in used:
            cnt[o["e"]] = cnt.get(o["e"], 0) + 1
            val[i] = cnt[o["e"]]
        elif o["sem"]:
            val[i] = o["sem"][1]
    nsend = 0
    for i in order:
        o = ops[i]
        if o["k"] == "r":
            continue
        e = eng[o["e"]]
        for s, j in need[i]:
            e.wait_ge(T.sem[s], val[j])
        ins = o["fn"](e)
        if o["k"] == "d":
            ins.then_inc(T.sem[o["sem"][0]], 16)
        elif o["k"] == "s":
            nsend += 1
        elif i in used:
            ins.then_inc(T.sem[esem[o["e"]]], 1)
    g.wait_ge(T.sem.ls, nsend * NE)
    for i in order:
        if ops[i]["k"] in "dr" and i not in used:
            g.sync.wait_ge(T.sem[ops[i]["sem"][0]], val[i])
